import numpy as np
import ml_dtypes


def mxq(x, axis, fmt="e4m3"):
    dtype, down = {"e4m3": (ml_dtypes.float8_e4m3fn, 7), "e5m2": (ml_dtypes.float8_e5m2, 14)}[fmt]
    v = np.moveaxis(np.asarray(x, np.float32).astype(ml_dtypes.bfloat16).astype(np.float64), axis, -1)
    blocks = v.reshape(v.shape[:-1] + (-1, 32))
    amax = np.abs(blocks).max(-1, keepdims=True)
    byte = np.maximum(np.where(amax > 0, np.frexp(amax)[1] - 1 + 127, 0) - down, 1)
    scale = np.exp2(byte - 127.0)
    codes = (blocks / scale).astype(np.float32).astype(dtype).astype(np.float64)
    return np.moveaxis((codes * scale).reshape(v.shape), -1, axis)


WIDE = False


def mx_kscale(k):
    if not WIDE:
        return np.ones(k)
    levels = np.array([10, -10, 5, -5, 0])
    if k % 512:
        return np.exp2(np.random.permutation(np.resize(levels, k // 32))).repeat(32)
    a = np.empty((k // 512, 16))
    for p in range(k // 512):
        a[p, :8] = np.random.permutation(np.resize(levels, 8))
        for g in range(8):
            far = levels[np.abs(levels - a[p, g]) >= 10]
            a[p, g + 8] = far[np.random.randint(len(far))]
    return np.exp2(a.ravel()).repeat(32)


def f64(x):
    return np.asarray(x).astype(np.float64)


def striped(idx):
    return np.tile(idx.reshape(-1, 16).T, (8, 1)).astype(np.uint16)


def unstriped(offs):
    return offs[:16].T.reshape(-1).astype(np.int64)


def pack_weight(w):
    k, n = w.shape
    w = f64(np.asarray(w, np.float32).astype(ml_dtypes.bfloat16)).reshape(k // 32, 32, n)
    amax = np.abs(w).max(1)
    byte = np.clip(np.where(amax > 0, np.frexp(amax)[1] - 1 + 127 - 7, 1), 1, 254)
    scaled = (w * np.exp2(127.0 - byte)[:, None, :]).reshape(k, n).astype(np.float32)
    words = np.ascontiguousarray(scaled.reshape(k // 512, 128, 4, n).transpose(0, 1, 3, 2)).astype(ml_dtypes.float8_e4m3fn).view(np.uint8)
    return words, np.ascontiguousarray(byte.astype(np.uint8).reshape(k // 512, 16, n))


def unpack_weight(words, scales):
    g, p, n, _ = words.shape
    vals = np.ascontiguousarray(words).view(ml_dtypes.float8_e4m3fn).astype(np.float64) * np.repeat(np.exp2(scales.astype(np.float64) - 127.0), 8, axis=1)[..., None]
    return vals.transpose(0, 1, 3, 2).reshape(g * 512, n)


K, T, S, V, R = 1024, 2048, 512, 512, 256
P = 2 ** 7


def setup_inputs():
    n = np.random.standard_normal
    s = mx_kscale(K)[:, None]
    packed_xT = pack_weight(n((K, T)) * s)
    return {
        "x_words": packed_xT[0],
        "x_scales": packed_xT[1],
        "hT": (n((K, V)) / np.sqrt(K) / s).astype(np.float32),
        "share": (np.tile(np.random.uniform(0.1, 0.9, R), (P, 1))).astype(np.float32),
        "inv": (np.tile(np.random.uniform(1.0, 1.4, R), (P, 1))).astype(np.float32),
        "offs": striped(np.random.permutation(T)[:S]),
        "one": striped(np.random.permutation(S)[:R]),
        "two": striped(np.random.permutation(S)[:R]),
    }


def reference(x_words, x_scales, hT, share, inv, offs, one, two):
    hTq = mxq(f64(hT), 0, "e4m3")
    xq = unpack_weight(x_words, x_scales)[:, unstriped(offs)]
    y = hTq.T @ xq
    p2 = y[:, unstriped(two)]
    syn = (p2 + f64(share)[:1] * (y[:, unstriped(one)] - p2)) * f64(inv)[:1]
    al = np.concatenate([y, syn], axis=1)
    ex = np.exp(al - al.max(axis=1, keepdims=True))
    return ex / ex.sum(axis=1, keepdims=True)

@@ -1,0 +1,185 @@
+from contextlib import ExitStack
+
+import concourse.mybir as mybir
+
+K, T, S, V, R = 1024, 2048, 512, 512, 256
+P = 128
+PACK = 4
+K_PASS = P * PACK
+PASSES = K // K_PASS
+TILES = V // P
+FLOPS = 2 * K * V * S
+
+F32 = mybir.dt.float32
+BF16 = mybir.dt.bfloat16
+I32 = mybir.dt.int32
+U32 = mybir.dt.uint32
+U16 = mybir.dt.uint16
+U8 = mybir.dt.uint8
+FP8X4 = mybir.dt.float8_e4m3fn_x4
+ALU = mybir.AluOpType
+ACT = mybir.ActivationFunctionType
+
+
+def tile_picked_ymochi_soft_p_kernel(
+    tc, x_words, x_scales, hT, share, inv, offs, one, two, out
+):
+    nc = tc.nc
+    with ExitStack() as ctx:
+        keep = ctx.enter_context(tc.tile_pool(name="keep", bufs=1))
+        psum = ctx.enter_context(tc.psum_pool(name="psum", bufs=1))
+
+        offs_t = keep.tile([P, S // 16], U16, name="offs_t")
+        one_t = keep.tile([P, R // 16], U16, name="one_t")
+        two_t = keep.tile([P, R // 16], U16, name="two_t")
+        words = [keep.tile([P, T], I32, name=f"words{o}", align_bytes=64) for o in range(PASSES)]
+        scale_rows = keep.tile([P, T], U8, name="scale_rows", align_bytes=64)
+        share_t = keep.tile([P, R], F32, name="share_t")
+        inv_t = keep.tile([P, R], F32, name="inv_t")
+
+        spans = [(0, 1), (1, 2), (2, 4)]
+        raw = {}
+        for first, last in spans:
+            for o in range(PASSES):
+                raw[first, o] = keep.tile([P, PACK, (last - first) * P], F32, name=f"raw{first}_{o}")
+
+        def load_words(o):
+            nc.sync.dma_start(out=words[o][:], in_=x_words[o].rearrange("p n t -> p (n t)").bitcast(I32))
+
+        def load_queries(first, last):
+            for o in range(PASSES):
+                rows = hT[o * K_PASS : (o + 1) * K_PASS, first * P : last * P]
+                nc.sync.dma_start(out=raw[first, o][:], in_=rows.rearrange("(p j) q -> p j q", j=PACK))
+
+        nc.vector.memset(scale_rows[:].bitcast(I32), 0)
+        nc.sync.dma_start(out=offs_t[:], in_=offs)
+        load_words(0)
+        for quad in range(4):
+            nc.scalar.dma_start(
+                out=scale_rows[32 * quad : 32 * quad + 4 * PASSES, :].bitcast(I32),
+                in_=x_scales[:, 4 * quad : 4 * quad + 4, :].bitcast(I32),
+            )
+        load_words(1)
+        load_queries(*spans[0])
+        nc.sync.dma_start(out=share_t[:], in_=share)
+        nc.sync.dma_start(out=inv_t[:], in_=inv)
+        nc.sync.dma_start(out=one_t[:], in_=one)
+        nc.sync.dma_start(out=two_t[:], in_=two)
+        load_queries(*spans[1])
+        load_queries(*spans[2])
+
+        picked_scales = keep.tile([P, S], U8, name="picked_scales", align_bytes=64)
+        picked = [keep.tile([P, S], U32, name=f"picked{o}", align_bytes=64) for o in range(PASSES)]
+        nc.vector.tensor_copy(out=picked[0][:], in_=words[0][:].bitcast(U32).indirect(offs_t[:]))
+        nc.vector.tensor_copy(out=picked_scales[:], in_=scale_rows[:].indirect(offs_t[:]))
+        nc.vector.tensor_copy(out=picked[1][:], in_=words[1][:].bitcast(U32).indirect(offs_t[:]))
+
+        grouped = [keep.tile([P, PASSES, P * PACK], BF16, name=f"grouped{i}", align_bytes=64) for i in range(TILES)]
+        h_codes = [keep.tile([P, PASSES * P], U32, name=f"h_codes{i}", align_bytes=64) for i in range(TILES)]
+        h_scales = [keep.tile([P, PASSES * P], U8, name=f"h_scales{i}", align_bytes=64) for i in range(TILES)]
+        banks = [psum.tile([P, S], F32, name=f"bank{i}") for i in range(TILES)]
+
+        def interleave(i, o, on_vector):
+            first = max(f for f, l in spans if f <= i)
+            src = raw[first, o][:, :, (i - first) * P : (i - first + 1) * P].rearrange("p j (c n) -> p c j n", n=4)
+            dst = grouped[i][:, o, :].rearrange("p (c n j) -> p c j n", n=4, j=PACK)
+            if on_vector:
+                nc.vector.tensor_copy(out=dst, in_=src)
+            else:
+                nc.scalar.copy(out=dst, in_=src)
+
+        def quantize(i, passes):
+            cols = slice(passes[0] * P, (passes[-1] + 1) * P)
+            nc.vector.quantize_mx(
+                out=h_codes[i][:, cols].bitcast(FP8X4),
+                scales=h_scales[i][:, cols],
+                in_=grouped[i][:, passes[0] : passes[-1] + 1, :].rearrange("p o w -> p (o w)"),
+            )
+
+        def multiply(i, o):
+            cols = slice(o * P, (o + 1) * P)
+            nc.tensor.matmul_mx(
+                out=banks[i][:],
+                lhsT=h_codes[i][:, cols].bitcast(FP8X4),
+                lhsT_scale=h_scales[i][:, cols],
+                rhs=picked[o][:].bitcast(FP8X4),
+                rhs_scale=picked_scales[4 * o :, :],
+                start=(o == 0),
+                stop=(o == PASSES - 1),
+            )
+
+        def product(i):
+            for o in range(PASSES):
+                interleave(i, o, False)
+            quantize(i, list(range(PASSES)))
+            for o in range(PASSES):
+                multiply(i, o)
+
+        for o in range(PASSES):
+            interleave(0, o, o == PASSES - 1)
+            quantize(0, [o])
+            multiply(0, o)
+
+        w_one = keep.tile([P, R], F32, name="w_one")
+        w_two = keep.tile([P, R], F32, name="w_two")
+        nc.vector.tensor_tensor(out=w_one[:], in0=share_t[:], in1=inv_t[:], op=ALU.mult)
+        nc.vector.tensor_tensor(out=w_two[:], in0=inv_t[:], in1=w_one[:], op=ALU.subtract)
+
+        logits = [keep.tile([P, S + R], F32, name=f"logits{i}") for i in range(TILES)]
+        part_one = [keep.tile([P, R], F32, name=f"part_one{i}") for i in range(TILES)]
+        part_two = [keep.tile([P, R], F32, name=f"part_two{i}") for i in range(TILES)]
+        probs = [keep.tile([P, S + R], F32, name=f"probs{i}") for i in range(TILES)]
+        result = [keep.tile([P, S + R], F32, name=f"result{i}") for i in range(TILES)]
+        unread = keep.tile([P, R], F32, name="unread")
+        max_y = [keep.tile([P, 1], F32, name=f"max_y{i}") for i in range(TILES)]
+        neg_max_y = [keep.tile([P, 1], F32, name=f"neg_max_y{i}") for i in range(TILES)]
+        neg_max = [keep.tile([P, 1], F32, name=f"neg_max{i}") for i in range(TILES)]
+        total = [keep.tile([P, 1], F32, name=f"total{i}") for i in range(TILES)]
+        inv_total = [keep.tile([P, 1], F32, name=f"inv_total{i}") for i in range(TILES)]
+
+        def fetch_scores(i):
+            nc.vector.tensor_scalar(
+                out=logits[i][:, :S], in0=banks[i][:], scalar1=1.0, scalar2=None,
+                op0=ALU.mult, op1=ALU.max, accum_out=max_y[i][:],
+            )
+            nc.gpsimd.tensor_scalar(
+                out=neg_max_y[i][:], in0=max_y[i][:], scalar1=-1.0, scalar2=0.0, op0=ALU.mult, op1=ALU.add
+            )
+
+        def mix(i):
+            nc.vector.tensor_tensor(out=part_one[i][:], in0=logits[i][:].indirect(one_t[:]), in1=w_one[:], op=ALU.mult)
+            nc.vector.tensor_tensor(out=part_two[i][:], in0=logits[i][:].indirect(two_t[:]), in1=w_two[:], op=ALU.mult)
+            adder = nc.vector if i == TILES - 1 else nc.gpsimd
+            adder.tensor_tensor(out=logits[i][:, S:], in0=part_one[i][:], in1=part_two[i][:], op=ALU.add)
+
+        def exponentials(i):
+            nc.vector.tensor_scalar(
+                out=unread[:], in0=logits[i][:, S:], scalar1=-1.0, scalar2=neg_max_y[i][:],
+                op0=ALU.mult, op1=ALU.min, accum_out=neg_max[i][:],
+            )
+            nc.scalar.activation(
+                out=probs[i][:], in_=logits[i][:], func=ACT.Exp, bias=neg_max[i][:], scale=1.0, accum_out=total[i][:]
+            )
+
+        def normalise(i):
+            nc.vector.reciprocal(out=inv_total[i][:], in_=total[i][:])
+            split = S if i == TILES - 1 else 0
+            if split:
+                nc.vector.tensor_scalar(
+                    out=result[i][:, :split], in0=probs[i][:, :split], scalar1=inv_total[i][:], scalar2=None, op0=ALU.mult
+                )
+            nc.scalar.activation(out=result[i][:, split:], in_=probs[i][:, split:], func=ACT.Copy, scale=inv_total[i][:])
+            nc.sync.dma_start(out=out[i * P : (i + 1) * P, :], in_=result[i][:])
+
+        product(1)
+        fetch_scores(0)
+        for i in range(TILES):
+            mix(i)
+            if i + 1 < TILES:
+                fetch_scores(i + 1)
+            exponentials(i)
+            if i + 2 < TILES:
+                product(i + 2)
+            if i >= 1:
+                normalise(i - 1)
+        normalise(TILES - 1)

@@ -37,7 +37,7 @@ def tile_picked_ymochi_soft_p_kernel(
         share_t = keep.tile([P, R], F32, name="share_t")
         inv_t = keep.tile([P, R], F32, name="inv_t")
 
-        spans = [(0, 1), (1, 2), (2, 4)]
+        spans = [(0, 1), (1, 2), (2, 3), (3, 4)]
         raw = {}
         for first, last in spans:
             for o in range(PASSES):
@@ -51,76 +51,60 @@ def tile_picked_ymochi_soft_p_kernel(
                 rows = hT[o * K_PASS : (o + 1) * K_PASS, first * P : last * P]
                 nc.sync.dma_start(out=raw[first, o][:], in_=rows.rearrange("(p j) q -> p j q", j=PACK))
 
-        nc.vector.memset(scale_rows[:].bitcast(I32), 0)
-        nc.sync.dma_start(out=offs_t[:], in_=offs)
-        load_words(0)
+        landed_rows = keep.tile([P, T], U8, name="landed_rows", align_bytes=64)
+        live = [slice(32 * quad, 32 * quad + 4 * PASSES) for quad in range(4)]
         for quad in range(4):
-            nc.scalar.dma_start(
-                out=scale_rows[32 * quad : 32 * quad + 4 * PASSES, :].bitcast(I32),
+            nc.sync.dma_start(
+                out=landed_rows[live[quad], :].bitcast(I32),
                 in_=x_scales[:, 4 * quad : 4 * quad + 4, :].bitcast(I32),
             )
+        nc.sync.dma_start(out=offs_t[:], in_=offs)
+        load_words(0)
         load_words(1)
         load_queries(*spans[0])
         nc.sync.dma_start(out=share_t[:], in_=share)
         nc.sync.dma_start(out=inv_t[:], in_=inv)
         nc.sync.dma_start(out=one_t[:], in_=one)
         nc.sync.dma_start(out=two_t[:], in_=two)
-        load_queries(*spans[1])
-        load_queries(*spans[2])
+        for span in spans[1:]:
+            load_queries(*span)
 
         picked_scales = keep.tile([P, S], U8, name="picked_scales", align_bytes=64)
         picked = [keep.tile([P, S], U32, name=f"picked{o}", align_bytes=64) for o in range(PASSES)]
-        nc.vector.tensor_copy(out=picked[0][:], in_=words[0][:].bitcast(U32).indirect(offs_t[:]))
+        nc.vector.memset(scale_rows[:].bitcast(I32), 0)
+        for quad in range(4):
+            nc.vector.tensor_copy(out=scale_rows[live[quad], :].bitcast(I32), in_=landed_rows[live[quad], :].bitcast(I32))
         nc.vector.tensor_copy(out=picked_scales[:], in_=scale_rows[:].indirect(offs_t[:]))
+        nc.vector.tensor_copy(out=picked[0][:], in_=words[0][:].bitcast(U32).indirect(offs_t[:]))
         nc.vector.tensor_copy(out=picked[1][:], in_=words[1][:].bitcast(U32).indirect(offs_t[:]))
 
-        grouped = [keep.tile([P, PASSES, P * PACK], BF16, name=f"grouped{i}", align_bytes=64) for i in range(TILES)]
-        h_codes = [keep.tile([P, PASSES * P], U32, name=f"h_codes{i}", align_bytes=64) for i in range(TILES)]
-        h_scales = [keep.tile([P, PASSES * P], U8, name=f"h_scales{i}", align_bytes=64) for i in range(TILES)]
+        pairs = [(i, o) for i in range(TILES) for o in range(PASSES)]
+        grouped = {(i, o): keep.tile([P, P * PACK], BF16, name=f"grouped{i}_{o}", align_bytes=64) for i, o in pairs}
+        h_codes = {(i, o): keep.tile([P, P], U32, name=f"h_codes{i}_{o}", align_bytes=64) for i, o in pairs}
+        h_scales = {(i, o): keep.tile([P, P], U8, name=f"h_scales{i}_{o}", align_bytes=64) for i, o in pairs}
         banks = [psum.tile([P, S], F32, name=f"bank{i}") for i in range(TILES)]
-
-        def interleave(i, o, on_vector):
-            first = max(f for f, l in spans if f <= i)
-            src = raw[first, o][:, :, (i - first) * P : (i - first + 1) * P].rearrange("p j (c n) -> p c j n", n=4)
-            dst = grouped[i][:, o, :].rearrange("p (c n j) -> p c j n", n=4, j=PACK)
-            if on_vector:
-                nc.vector.tensor_copy(out=dst, in_=src)
-            else:
-                nc.scalar.copy(out=dst, in_=src)
-
-        def quantize(i, passes):
-            cols = slice(passes[0] * P, (passes[-1] + 1) * P)
-            nc.vector.quantize_mx(
-                out=h_codes[i][:, cols].bitcast(FP8X4),
-                scales=h_scales[i][:, cols],
-                in_=grouped[i][:, passes[0] : passes[-1] + 1, :].rearrange("p o w -> p (o w)"),
-            )
-
-        def multiply(i, o):
-            cols = slice(o * P, (o + 1) * P)
-            nc.tensor.matmul_mx(
-                out=banks[i][:],
-                lhsT=h_codes[i][:, cols].bitcast(FP8X4),
-                lhsT_scale=h_scales[i][:, cols],
-                rhs=picked[o][:].bitcast(FP8X4),
-                rhs_scale=picked_scales[4 * o :, :],
-                start=(o == 0),
-                stop=(o == PASSES - 1),
-            )
 
         def product(i):
             for o in range(PASSES):
-                interleave(i, o, False)
-            quantize(i, list(range(PASSES)))
-            for o in range(PASSES):
-                multiply(i, o)
+                nc.scalar.copy(
+                    out=grouped[i, o][:].rearrange("p (c n j) -> p c j n", n=4, j=PACK),
+                    in_=raw[i, o][:].rearrange("p j (c n) -> p c j n", n=4),
+                )
+                nc.vector.quantize_mx(
+                    out=h_codes[i, o][:].bitcast(FP8X4), scales=h_scales[i, o][:], in_=grouped[i, o][:]
+                )
+                nc.tensor.matmul_mx(
+                    out=banks[i][:],
+                    lhsT=h_codes[i, o][:].bitcast(FP8X4),
+                    lhsT_scale=h_scales[i, o][:],
+                    rhs=picked[o][:].bitcast(FP8X4),
+                    rhs_scale=picked_scales[4 * o :, :],
+                    start=(o == 0),
+                    stop=(o == PASSES - 1),
+                )
 
-        for o in range(PASSES):
-            interleave(0, o, o == PASSES - 1)
-            quantize(0, [o])
-            multiply(0, o)
-
-        w_one = keep.tile([P, R], F32, name="w_one")
+        product(0)
+        w_one = keep.tile([P, R], F32, name="w_one", tag=f"grouped0_{PASSES - 1}", align_bytes=64)
         w_two = keep.tile([P, R], F32, name="w_two")
         nc.vector.tensor_tensor(out=w_one[:], in0=share_t[:], in1=inv_t[:], op=ALU.mult)
         nc.vector.tensor_tensor(out=w_two[:], in0=inv_t[:], in1=w_one[:], op=ALU.subtract)
@@ -149,7 +133,7 @@ def tile_picked_ymochi_soft_p_kernel(
         def mix(i):
             nc.vector.tensor_tensor(out=part_one[i][:], in0=logits[i][:].indirect(one_t[:]), in1=w_one[:], op=ALU.mult)
             nc.vector.tensor_tensor(out=part_two[i][:], in0=logits[i][:].indirect(two_t[:]), in1=w_two[:], op=ALU.mult)
-            adder = nc.vector if i == TILES - 1 else nc.gpsimd
+            adder = nc.vector
             adder.tensor_tensor(out=logits[i][:, S:], in0=part_one[i][:], in1=part_two[i][:], op=ALU.add)
 
         def exponentials(i):

@@ -46,10 +46,9 @@ def tile_picked_ymochi_soft_p_kernel(
         def load_words(o):
             nc.sync.dma_start(out=words[o][:], in_=x_words[o].rearrange("p n t -> p (n t)").bitcast(I32))
 
-        def load_queries(first, last):
-            for o in range(PASSES):
-                rows = hT[o * K_PASS : (o + 1) * K_PASS, first * P : last * P]
-                nc.sync.dma_start(out=raw[first, o][:], in_=rows.rearrange("(p j) q -> p j q", j=PACK))
+        def load_queries(i, o):
+            rows = hT[o * K_PASS : (o + 1) * K_PASS, i * P : (i + 1) * P]
+            nc.sync.dma_start(out=raw[i, o][:], in_=rows.rearrange("(p j) q -> p j q", j=PACK))
 
         landed_rows = keep.tile([P, T], U8, name="landed_rows", align_bytes=64)
         live = [slice(32 * quad, 32 * quad + 4 * PASSES) for quad in range(4)]
@@ -59,15 +58,18 @@ def tile_picked_ymochi_soft_p_kernel(
                 in_=x_scales[:, 4 * quad : 4 * quad + 4, :].bitcast(I32),
             )
         nc.sync.dma_start(out=offs_t[:], in_=offs)
-        load_words(0)
-        load_words(1)
-        load_queries(*spans[0])
+        for o in range(PASSES):
+            load_words(o)
+            load_queries(0, o)
+        load_queries(1, 0)
         nc.sync.dma_start(out=share_t[:], in_=share)
         nc.sync.dma_start(out=inv_t[:], in_=inv)
         nc.sync.dma_start(out=one_t[:], in_=one)
         nc.sync.dma_start(out=two_t[:], in_=two)
-        for span in spans[1:]:
-            load_queries(*span)
+        load_queries(1, 1)
+        for i in range(2, TILES):
+            for o in range(PASSES):
+                load_queries(i, o)
 
         picked_scales = keep.tile([P, S], U8, name="picked_scales", align_bytes=64)
         picked = [keep.tile([P, S], U32, name=f"picked{o}", align_bytes=64) for o in range(PASSES)]
@@ -79,17 +81,22 @@ def tile_picked_ymochi_soft_p_kernel(
         nc.vector.tensor_copy(out=picked[1][:], in_=words[1][:].bitcast(U32).indirect(offs_t[:]))
 
         pairs = [(i, o) for i in range(TILES) for o in range(PASSES)]
-        grouped = {(i, o): keep.tile([P, P * PACK], BF16, name=f"grouped{i}_{o}", align_bytes=64) for i, o in pairs}
-        h_codes = {(i, o): keep.tile([P, P], U32, name=f"h_codes{i}_{o}", align_bytes=64) for i, o in pairs}
+        grouped = {}
+        h_codes = {}
         h_scales = {(i, o): keep.tile([P, P], U8, name=f"h_scales{i}_{o}", align_bytes=64) for i, o in pairs}
         banks = [psum.tile([P, S], F32, name=f"bank{i}") for i in range(TILES)]
 
-        def product(i):
+        def interleave(i):
             for o in range(PASSES):
+                grouped[i, o] = keep.tile([P, P * PACK], BF16, name=f"grouped{i}_{o}", align_bytes=64)
                 nc.scalar.copy(
                     out=grouped[i, o][:].rearrange("p (c n j) -> p c j n", n=4, j=PACK),
                     in_=raw[i, o][:].rearrange("p j (c n) -> p c j n", n=4),
                 )
+
+        def product(i):
+            for o in range(PASSES):
+                h_codes[i, o] = keep.tile([P, P], U32, name=f"h_codes{i}_{o}", align_bytes=64)
                 nc.vector.quantize_mx(
                     out=h_codes[i, o][:].bitcast(FP8X4), scales=h_scales[i, o][:], in_=grouped[i, o][:]
                 )
@@ -103,67 +110,75 @@ def tile_picked_ymochi_soft_p_kernel(
                     stop=(o == PASSES - 1),
                 )
 
+        for i in range(TILES):
+            interleave(i)
         product(0)
-        w_one = keep.tile([P, R], F32, name="w_one", tag=f"grouped0_{PASSES - 1}", align_bytes=64)
+        w_one = keep.tile([P, R], F32, name="w_one")
         w_two = keep.tile([P, R], F32, name="w_two")
         nc.vector.tensor_tensor(out=w_one[:], in0=share_t[:], in1=inv_t[:], op=ALU.mult)
-        nc.vector.tensor_tensor(out=w_two[:], in0=inv_t[:], in1=w_one[:], op=ALU.subtract)
+        nc.vector.scalar_tensor_tensor(
+            out=w_two[:], in0=share_t[:], scalar=1.0, in1=inv_t[:], op0=ALU.subtract, op1=ALU.mult
+        )
 
-        logits = [keep.tile([P, S + R], F32, name=f"logits{i}") for i in range(TILES)]
-        part_one = [keep.tile([P, R], F32, name=f"part_one{i}") for i in range(TILES)]
-        part_two = [keep.tile([P, R], F32, name=f"part_two{i}") for i in range(TILES)]
-        probs = [keep.tile([P, S + R], F32, name=f"probs{i}") for i in range(TILES)]
+        logits = [keep.tile([P, S + R], F32, name=f"logits{i}", align_bytes=64) for i in range(TILES)]
+        parts = {}
+        probs = {}
         result = [keep.tile([P, S + R], F32, name=f"result{i}") for i in range(TILES)]
-        unread = keep.tile([P, R], F32, name="unread")
-        max_y = [keep.tile([P, 1], F32, name=f"max_y{i}") for i in range(TILES)]
+        mixed = {}
         neg_max_y = [keep.tile([P, 1], F32, name=f"neg_max_y{i}") for i in range(TILES)]
         neg_max = [keep.tile([P, 1], F32, name=f"neg_max{i}") for i in range(TILES)]
-        total = [keep.tile([P, 1], F32, name=f"total{i}") for i in range(TILES)]
+        total = {}
         inv_total = [keep.tile([P, 1], F32, name=f"inv_total{i}") for i in range(TILES)]
 
         def fetch_scores(i):
             nc.vector.tensor_scalar(
-                out=logits[i][:, :S], in0=banks[i][:], scalar1=1.0, scalar2=None,
-                op0=ALU.mult, op1=ALU.max, accum_out=max_y[i][:],
-            )
-            nc.gpsimd.tensor_scalar(
-                out=neg_max_y[i][:], in0=max_y[i][:], scalar1=-1.0, scalar2=0.0, op0=ALU.mult, op1=ALU.add
+                out=logits[i][:, :S], in0=banks[i][:], scalar1=-1.0, scalar2=None,
+                op0=ALU.mult, op1=ALU.min, accum_out=neg_max_y[i][:],
             )
 
         def mix(i):
-            nc.vector.tensor_tensor(out=part_one[i][:], in0=logits[i][:].indirect(one_t[:]), in1=w_one[:], op=ALU.mult)
-            nc.vector.tensor_tensor(out=part_two[i][:], in0=logits[i][:].indirect(two_t[:]), in1=w_two[:], op=ALU.mult)
-            adder = nc.vector
-            adder.tensor_tensor(out=logits[i][:, S:], in0=part_one[i][:], in1=part_two[i][:], op=ALU.add)
+            tag = f"grouped{i + 1}_{PASSES - 1}" if i + 1 < TILES else "last_parts"
+            parts[i] = keep.tile([P, 2 * R], F32, name=f"parts{i}", tag=tag, align_bytes=64)
+            nc.vector.tensor_tensor(out=parts[i][:, :R], in0=logits[i][:].indirect(one_t[:]), in1=w_one[:], op=ALU.mult)
+            nc.vector.tensor_tensor(out=parts[i][:, R:], in0=logits[i][:].indirect(two_t[:]), in1=w_two[:], op=ALU.mult)
+
+        def join(i):
+            mixed[i] = keep.tile([P, R], F32, name=f"mixed{i}")
+            nc.vector.tensor_tensor(out=mixed[i][:], in0=parts[i][:, :R], in1=parts[i][:, R:], op=ALU.subtract)
 
         def exponentials(i):
             nc.vector.tensor_scalar(
-                out=unread[:], in0=logits[i][:, S:], scalar1=-1.0, scalar2=neg_max_y[i][:],
+                out=logits[i][:, S:], in0=mixed[i][:], scalar1=1.0, scalar2=neg_max_y[i][:],
                 op0=ALU.mult, op1=ALU.min, accum_out=neg_max[i][:],
             )
+            probs[i] = keep.tile([P, S + R], F32, name=f"probs{i}")
+            total[i] = keep.tile([P, 1], F32, name=f"total{i}")
             nc.scalar.activation(
-                out=probs[i][:], in_=logits[i][:], func=ACT.Exp, bias=neg_max[i][:], scale=1.0, accum_out=total[i][:]
+                out=probs[i][:], in_=logits[i][:], func=ACT.Exp, bias=neg_max[i][:], scale=-1.0, accum_out=total[i][:]
             )
 
         def normalise(i):
             nc.vector.reciprocal(out=inv_total[i][:], in_=total[i][:])
-            split = S if i == TILES - 1 else 0
+            split = {TILES - 2: S + R, TILES - 1: S}.get(i, 0)
             if split:
                 nc.vector.tensor_scalar(
                     out=result[i][:, :split], in0=probs[i][:, :split], scalar1=inv_total[i][:], scalar2=None, op0=ALU.mult
                 )
-            nc.scalar.activation(out=result[i][:, split:], in_=probs[i][:, split:], func=ACT.Copy, scale=inv_total[i][:])
+            if split < S + R:
+                nc.scalar.activation(out=result[i][:, split:], in_=probs[i][:, split:], func=ACT.Copy, scale=inv_total[i][:])
             nc.sync.dma_start(out=out[i * P : (i + 1) * P, :], in_=result[i][:])
 
         product(1)
         fetch_scores(0)
         for i in range(TILES):
+            if 1 <= i < TILES - 1:
+                product(i + 1)
             mix(i)
+            if 1 <= i < TILES - 1:
+                normalise(i - 1)
             if i + 1 < TILES:
                 fetch_scores(i + 1)
+            join(i)
             exponentials(i)
-            if i + 2 < TILES:
-                product(i + 2)
-            if i >= 1:
-                normalise(i - 1)
+        normalise(TILES - 2)
         normalise(TILES - 1)

@@ -8,6 +8,9 @@ PACK = 4
 K_PASS = P * PACK
 PASSES = K // K_PASS
 TILES = V // P
+QUADS = 4
+SCALE_ROWS = 4
+RUN = 4
 FLOPS = 2 * K * V * S
 
 F32 = mybir.dt.float32
@@ -28,6 +31,7 @@ def tile_picked_ymochi_soft_p_kernel(
     with ExitStack() as ctx:
         keep = ctx.enter_context(tc.tile_pool(name="keep", bufs=1))
         psum = ctx.enter_context(tc.psum_pool(name="psum", bufs=1))
+        pairs = [(i, o) for i in range(TILES) for o in range(PASSES)]
 
         offs_t = keep.tile([P, S // 16], U16, name="offs_t")
         one_t = keep.tile([P, R // 16], U16, name="one_t")
@@ -36,12 +40,7 @@ def tile_picked_ymochi_soft_p_kernel(
         scale_rows = keep.tile([P, T], U8, name="scale_rows", align_bytes=64)
         share_t = keep.tile([P, R], F32, name="share_t")
         inv_t = keep.tile([P, R], F32, name="inv_t")
-
-        spans = [(0, 1), (1, 2), (2, 3), (3, 4)]
-        raw = {}
-        for first, last in spans:
-            for o in range(PASSES):
-                raw[first, o] = keep.tile([P, PACK, (last - first) * P], F32, name=f"raw{first}_{o}")
+        raw = {(i, o): keep.tile([P, PACK, P], F32, name=f"raw{i}_{o}") for i, o in pairs}
 
         def load_words(o):
             nc.sync.dma_start(out=words[o][:], in_=x_words[o].rearrange("p n t -> p (n t)").bitcast(I32))
@@ -51,11 +50,11 @@ def tile_picked_ymochi_soft_p_kernel(
             nc.sync.dma_start(out=raw[i, o][:], in_=rows.rearrange("(p j) q -> p j q", j=PACK))
 
         landed_rows = keep.tile([P, T], U8, name="landed_rows", align_bytes=64)
-        live = [slice(32 * quad, 32 * quad + 4 * PASSES) for quad in range(4)]
-        for quad in range(4):
-            nc.sync.dma_start(
+        live = [slice(32 * quad, 32 * quad + SCALE_ROWS * PASSES) for quad in range(QUADS)]
+        for quad in range(QUADS):
+            (nc.scalar if quad < QUADS // 2 else nc.sync).dma_start(
                 out=landed_rows[live[quad], :].bitcast(I32),
-                in_=x_scales[:, 4 * quad : 4 * quad + 4, :].bitcast(I32),
+                in_=x_scales[:, SCALE_ROWS * quad : SCALE_ROWS * (quad + 1), :].bitcast(I32),
             )
         nc.sync.dma_start(out=offs_t[:], in_=offs)
         for o in range(PASSES):
@@ -74,13 +73,12 @@ def tile_picked_ymochi_soft_p_kernel(
         picked_scales = keep.tile([P, S], U8, name="picked_scales", align_bytes=64)
         picked = [keep.tile([P, S], U32, name=f"picked{o}", align_bytes=64) for o in range(PASSES)]
         nc.vector.memset(scale_rows[:].bitcast(I32), 0)
-        for quad in range(4):
+        for quad in range(QUADS):
             nc.vector.tensor_copy(out=scale_rows[live[quad], :].bitcast(I32), in_=landed_rows[live[quad], :].bitcast(I32))
         nc.vector.tensor_copy(out=picked_scales[:], in_=scale_rows[:].indirect(offs_t[:]))
-        nc.vector.tensor_copy(out=picked[0][:], in_=words[0][:].bitcast(U32).indirect(offs_t[:]))
-        nc.vector.tensor_copy(out=picked[1][:], in_=words[1][:].bitcast(U32).indirect(offs_t[:]))
+        for o in range(PASSES):
+            nc.vector.tensor_copy(out=picked[o][:], in_=words[o][:].bitcast(U32).indirect(offs_t[:]))
 
-        pairs = [(i, o) for i in range(TILES) for o in range(PASSES)]
         grouped = {}
         h_codes = {}
         h_scales = {(i, o): keep.tile([P, P], U8, name=f"h_scales{i}_{o}", align_bytes=64) for i, o in pairs}
@@ -90,8 +88,8 @@ def tile_picked_ymochi_soft_p_kernel(
             for o in range(PASSES):
                 grouped[i, o] = keep.tile([P, P * PACK], BF16, name=f"grouped{i}_{o}", align_bytes=64)
                 nc.scalar.copy(
-                    out=grouped[i, o][:].rearrange("p (c n j) -> p c j n", n=4, j=PACK),
-                    in_=raw[i, o][:].rearrange("p j (c n) -> p c j n", n=4),
+                    out=grouped[i, o][:].rearrange("p (c n j) -> p c j n", n=RUN, j=PACK),
+                    in_=raw[i, o][:].rearrange("p j (c n) -> p c j n", n=RUN),
                 )
 
         def product(i):
@@ -105,7 +103,7 @@ def tile_picked_ymochi_soft_p_kernel(
                     lhsT=h_codes[i, o][:].bitcast(FP8X4),
                     lhsT_scale=h_scales[i, o][:],
                     rhs=picked[o][:].bitcast(FP8X4),
-                    rhs_scale=picked_scales[4 * o :, :],
+                    rhs_scale=picked_scales[SCALE_ROWS * o :, :],
                     start=(o == 0),
                     stop=(o == PASSES - 1),
                 )
@@ -113,6 +111,7 @@ def tile_picked_ymochi_soft_p_kernel(
         for i in range(TILES):
             interleave(i)
         product(0)
+
         w_one = keep.tile([P, R], F32, name="w_one")
         w_two = keep.tile([P, R], F32, name="w_two")
         nc.vector.tensor_tensor(out=w_one[:], in0=share_t[:], in1=inv_t[:], op=ALU.mult)
@@ -121,7 +120,8 @@ def tile_picked_ymochi_soft_p_kernel(
         )
 
         logits = [keep.tile([P, S + R], F32, name=f"logits{i}", align_bytes=64) for i in range(TILES)]
-        parts = {}
+        part_one = {}
+        part_two = {}
         probs = {}
         result = [keep.tile([P, S + R], F32, name=f"result{i}") for i in range(TILES)]
         mixed = {}
@@ -138,13 +138,14 @@ def tile_picked_ymochi_soft_p_kernel(
 
         def mix(i):
             tag = f"grouped{i + 1}_{PASSES - 1}" if i + 1 < TILES else "last_parts"
-            parts[i] = keep.tile([P, 2 * R], F32, name=f"parts{i}", tag=tag, align_bytes=64)
-            nc.vector.tensor_tensor(out=parts[i][:, :R], in0=logits[i][:].indirect(one_t[:]), in1=w_one[:], op=ALU.mult)
-            nc.vector.tensor_tensor(out=parts[i][:, R:], in0=logits[i][:].indirect(two_t[:]), in1=w_two[:], op=ALU.mult)
+            part_one[i] = keep.tile([P, R], F32, name=f"part_one{i}")
+            part_two[i] = keep.tile([P, R], F32, name=f"part_two{i}", tag=tag, align_bytes=64)
+            nc.vector.tensor_tensor(out=part_one[i][:], in0=logits[i][:].indirect(one_t[:]), in1=w_one[:], op=ALU.mult)
+            nc.vector.tensor_tensor(out=part_two[i][:], in0=logits[i][:].indirect(two_t[:]), in1=w_two[:], op=ALU.mult)
 
         def join(i):
             mixed[i] = keep.tile([P, R], F32, name=f"mixed{i}")
-            nc.vector.tensor_tensor(out=mixed[i][:], in0=parts[i][:, :R], in1=parts[i][:, R:], op=ALU.subtract)
+            nc.vector.tensor_tensor(out=mixed[i][:], in0=part_one[i][:], in1=part_two[i][:], op=ALU.subtract)
 
         def exponentials(i):
             nc.vector.tensor_scalar(
@@ -159,7 +160,7 @@ def tile_picked_ymochi_soft_p_kernel(
 
         def normalise(i):
             nc.vector.reciprocal(out=inv_total[i][:], in_=total[i][:])
-            split = {TILES - 2: S + R, TILES - 1: S}.get(i, 0)
+            split = {TILES - 2: S + R, TILES - 1: 2 * (S + R) // 3}.get(i, 0)
             if split:
                 nc.vector.tensor_scalar(
                     out=result[i][:, :split], in0=probs[i][:, :split], scalar1=inv_total[i][:], scalar2=None, op0=ALU.mult

@@ -1,6 +1,7 @@
 from contextlib import ExitStack
 
 import concourse.mybir as mybir
+from concourse.masks import make_identity
 
 K, T, S, V, R = 1024, 2048, 512, 512, 256
 P = 128
@@ -11,6 +12,7 @@ TILES = V // P
 QUADS = 4
 SCALE_ROWS = 4
 RUN = 4
+PAD = 8
 FLOPS = 2 * K * V * S
 
 F32 = mybir.dt.float32
@@ -38,9 +40,9 @@ def tile_picked_ymochi_soft_p_kernel(
         two_t = keep.tile([P, R // 16], U16, name="two_t")
         words = [keep.tile([P, T], I32, name=f"words{o}", align_bytes=64) for o in range(PASSES)]
         scale_rows = keep.tile([P, T], U8, name="scale_rows", align_bytes=64)
-        share_t = keep.tile([P, R], F32, name="share_t")
-        inv_t = keep.tile([P, R], F32, name="inv_t")
-        raw = {(i, o): keep.tile([P, PACK, P], F32, name=f"raw{i}_{o}") for i, o in pairs}
+        share_t = keep.tile([P, R // P], F32, name="share_t")
+        inv_t = keep.tile([P, R // P], F32, name="inv_t")
+        raw = {(i, o): keep.tile([P, PACK, P], F32, name=f"raw{i}_{o}", align_bytes=64) for i, o in pairs}
 
         def load_words(o):
             nc.sync.dma_start(out=words[o][:], in_=x_words[o].rearrange("p n t -> p (n t)").bitcast(I32))
@@ -57,16 +59,15 @@ def tile_picked_ymochi_soft_p_kernel(
                 in_=x_scales[:, SCALE_ROWS * quad : SCALE_ROWS * (quad + 1), :].bitcast(I32),
             )
         nc.sync.dma_start(out=offs_t[:], in_=offs)
+        for tile, rows in ((share_t, share), (inv_t, inv)):
+            nc.sync.dma_start(out=tile[:], in_=rows[0, :].rearrange("(p c) -> p c", p=P))
         for o in range(PASSES):
             load_words(o)
+        for o in range(PASSES):
             load_queries(0, o)
-        load_queries(1, 0)
-        nc.sync.dma_start(out=share_t[:], in_=share)
-        nc.sync.dma_start(out=inv_t[:], in_=inv)
         nc.sync.dma_start(out=one_t[:], in_=one)
         nc.sync.dma_start(out=two_t[:], in_=two)
-        load_queries(1, 1)
-        for i in range(2, TILES):
+        for i in range(1, TILES):
             for o in range(PASSES):
                 load_queries(i, o)
 
@@ -79,107 +80,235 @@ def tile_picked_ymochi_soft_p_kernel(
         for o in range(PASSES):
             nc.vector.tensor_copy(out=picked[o][:], in_=words[o][:].bitcast(U32).indirect(offs_t[:]))
 
-        grouped = {}
+        per = R // P
+        identity = keep.tile([P, P], F32, name="identity")
+        make_identity(nc, identity[:])
+        columns_w = keep.tile([P, 2 * per], F32, name="columns_w")
+        nc.vector.tensor_tensor(out=columns_w[:, :per], in0=share_t[:], in1=inv_t[:], op=ALU.mult)
+        nc.vector.scalar_tensor_tensor(
+            out=columns_w[:, per:], in0=share_t[:], scalar=1.0, in1=inv_t[:], op0=ALU.subtract, op1=ALU.mult
+        )
+        spread = psum.tile([P, 2 * per, P], F32, name="spread")
+        for n in range(2 * per):
+            nc.tensor.transpose(spread[:, n, :], columns_w[:, n : n + 1].to_broadcast([P, P]), identity[:])
+        weights = keep.tile([P, 2 * R], F32, name="weights")
+        nc.scalar.copy(
+            out=weights[:].rearrange("q (t p c) -> q t p c", t=2, c=per),
+            in_=spread[:].rearrange("q (t c) p -> q t p c", t=2),
+        )
+        w_one = weights[:, :R]
+        w_two = weights[:, R:]
+
+        grouped = [keep.tile([P, PASSES * K_PASS], BF16, name=f"grouped{i}", align_bytes=64) for i in range(TILES)]
         h_codes = {}
-        h_scales = {(i, o): keep.tile([P, P], U8, name=f"h_scales{i}_{o}", align_bytes=64) for i, o in pairs}
-        banks = [psum.tile([P, S], F32, name=f"bank{i}") for i in range(TILES)]
+        h_scales = {}
+        spans = {i: [(0, S // 2), (S // 2, S)] if i == 0 else [(0, S)] for i in range(TILES)}
+        banks = {
+            (i, first): psum.tile([P, end - first], F32, name=f"bank{i}_{first}")
+            for i in range(TILES)
+            for first, end in spans[i]
+        }
 
-        def interleave(i):
-            for o in range(PASSES):
-                grouped[i, o] = keep.tile([P, P * PACK], BF16, name=f"grouped{i}_{o}", align_bytes=64)
-                nc.scalar.copy(
-                    out=grouped[i, o][:].rearrange("p (c n j) -> p c j n", n=RUN, j=PACK),
-                    in_=raw[i, o][:].rearrange("p j (c n) -> p c j n", n=RUN),
-                )
+        def interleave(copy, i, o, first, last):
+            copy(
+                out=grouped[i][:, o * K_PASS + PACK * first : o * K_PASS + PACK * last].rearrange(
+                    "p (c n j) -> p c j n", n=RUN, j=PACK
+                ),
+                in_=raw[i, o][:, :, first:last].rearrange("p j (c n) -> p c j n", n=RUN),
+            )
 
-        def product(i):
-            for o in range(PASSES):
-                h_codes[i, o] = keep.tile([P, P], U32, name=f"h_codes{i}_{o}", align_bytes=64)
-                nc.vector.quantize_mx(
-                    out=h_codes[i, o][:].bitcast(FP8X4), scales=h_scales[i, o][:], in_=grouped[i, o][:]
-                )
+        def quantise(i, first, last):
+            tag = {(0, 0): "scales_a", (0, 1): "scales_b", (1, 0): "scales_d"}.get((i, first), "raw2_1" if i == 3 else "scales_c")
+            plane = keep.tile([P, (last - first) * P], U8, name=f"h_scales{i}_{first}", tag=tag, align_bytes=64)
+            name = f"h_codes{i}" if last == PASSES else f"early_codes{i}"
+            codes = keep.tile([P, (last - first) * P], U32, name=name, align_bytes=64)
+            for o in range(first, last):
+                h_codes[i, o] = codes[:, (o - first) * P : (o - first + 1) * P]
+                h_scales[i, o] = plane[:, (o - first) * P : (o - first + 1) * P]
+            nc.vector.quantize_mx(
+                out=codes[:].bitcast(FP8X4),
+                scales=plane[:],
+                in_=grouped[i][:, first * K_PASS : last * K_PASS],
+            )
+
+        def multiply(i, o):
+            for first, end in spans[i]:
                 nc.tensor.matmul_mx(
-                    out=banks[i][:],
-                    lhsT=h_codes[i, o][:].bitcast(FP8X4),
-                    lhsT_scale=h_scales[i, o][:],
-                    rhs=picked[o][:].bitcast(FP8X4),
-                    rhs_scale=picked_scales[SCALE_ROWS * o :, :],
+                    out=banks[i, first][:],
+                    lhsT=h_codes[i, o].bitcast(FP8X4),
+                    lhsT_scale=h_scales[i, o],
+                    rhs=picked[o][:, first:end].bitcast(FP8X4),
+                    rhs_scale=picked_scales[SCALE_ROWS * o :, first:end],
                     start=(o == 0),
                     stop=(o == PASSES - 1),
                 )
 
-        for i in range(TILES):
-            interleave(i)
-        product(0)
+        for i, o in pairs:
+            if (i, o) == (0, PASSES - 1):
+                interleave(nc.scalar.copy, i, o, 0, P // 2)
+                interleave(nc.vector.tensor_copy, i, o, P // 2, P)
+            else:
+                interleave(nc.scalar.copy, i, o, 0, P)
+        for o in range(PASSES):
+            quantise(0, o, o + 1)
+            multiply(0, o)
 
-        w_one = keep.tile([P, R], F32, name="w_one")
-        w_two = keep.tile([P, R], F32, name="w_two")
-        nc.vector.tensor_tensor(out=w_one[:], in0=share_t[:], in1=inv_t[:], op=ALU.mult)
-        nc.vector.scalar_tensor_tensor(
-            out=w_two[:], in0=share_t[:], scalar=1.0, in1=inv_t[:], op0=ALU.subtract, op1=ALU.mult
-        )
-
-        logits = [keep.tile([P, S + R], F32, name=f"logits{i}", align_bytes=64) for i in range(TILES)]
+        last = TILES - 1
+        low = slice(S + R, S + R + 1)
+        logits = {}
         part_one = {}
         part_two = {}
-        probs = {}
-        result = [keep.tile([P, S + R], F32, name=f"result{i}") for i in range(TILES)]
         mixed = {}
-        neg_max_y = [keep.tile([P, 1], F32, name=f"neg_max_y{i}") for i in range(TILES)]
-        neg_max = [keep.tile([P, 1], F32, name=f"neg_max{i}") for i in range(TILES)]
+        probs = {}
+        neg_max = {}
         total = {}
-        inv_total = [keep.tile([P, 1], F32, name=f"inv_total{i}") for i in range(TILES)]
+        inv_total = {}
+        result = [keep.tile([P, S + R], F32, name=f"result{i}") for i in range(TILES)]
 
-        def fetch_scores(i):
+        def held(name, tag):
+            tile = keep.tile([P, R + PAD], F32, name=name, tag=tag, align_bytes=64)
+            return tile[:, :R], tile[:, R : R + 1]
+
+        def column(name, tag=None):
+            return keep.tile([P, 1], F32, name=name, tag=tag or name, align_bytes=64)[:]
+
+        def fetch_scores(i, n=0):
+            if n == 0:
+                logits[i] = keep.tile([P, S + R + PAD], F32, name=f"logits{i}", tag=f"logits{i % 2}", align_bytes=64)
+            first, end = spans[i][n]
             nc.vector.tensor_scalar(
-                out=logits[i][:, :S], in0=banks[i][:], scalar1=-1.0, scalar2=None,
-                op0=ALU.mult, op1=ALU.min, accum_out=neg_max_y[i][:],
+                out=logits[i][:, first:end], in0=banks[i, first][:], scalar1=-1.0, scalar2=None,
+                op0=ALU.mult, op1=ALU.min, accum_out=half_low[n] if i == 0 else logits[i][:, low],
             )
 
-        def mix(i):
-            tag = f"grouped{i + 1}_{PASSES - 1}" if i + 1 < TILES else "last_parts"
-            part_one[i] = keep.tile([P, R], F32, name=f"part_one{i}")
-            part_two[i] = keep.tile([P, R], F32, name=f"part_two{i}", tag=tag, align_bytes=64)
-            nc.vector.tensor_tensor(out=part_one[i][:], in0=logits[i][:].indirect(one_t[:]), in1=w_one[:], op=ALU.mult)
-            nc.vector.tensor_tensor(out=part_two[i][:], in0=logits[i][:].indirect(two_t[:]), in1=w_two[:], op=ALU.mult)
+        def mix_one(i):
+            nc.vector.tensor_tensor(out=part_one[i], in0=logits[i][:].indirect(one_t[:]), in1=w_one, op=ALU.mult)
+
+        def mix_two(i):
+            nc.vector.tensor_tensor(out=part_two[i], in0=logits[i][:].indirect(two_t[:]), in1=w_two, op=ALU.mult)
 
         def join(i):
-            mixed[i] = keep.tile([P, R], F32, name=f"mixed{i}")
-            nc.vector.tensor_tensor(out=mixed[i][:], in0=part_one[i][:], in1=part_two[i][:], op=ALU.subtract)
+            target = mixed.get(i, logits[i][:, S : S + R])
+            nc.vector.tensor_tensor(out=target, in0=part_one[i], in1=part_two[i], op=ALU.subtract)
 
-        def exponentials(i):
-            nc.vector.tensor_scalar(
-                out=logits[i][:, S:], in0=mixed[i][:], scalar1=1.0, scalar2=neg_max_y[i][:],
-                op0=ALU.mult, op1=ALU.min, accum_out=neg_max[i][:],
-            )
-            probs[i] = keep.tile([P, S + R], F32, name=f"probs{i}")
-            total[i] = keep.tile([P, 1], F32, name=f"total{i}")
-            nc.scalar.activation(
-                out=probs[i][:], in_=logits[i][:], func=ACT.Exp, bias=neg_max[i][:], scale=-1.0, accum_out=total[i][:]
-            )
-
-        def normalise(i):
-            nc.vector.reciprocal(out=inv_total[i][:], in_=total[i][:])
-            split = {TILES - 2: S + R, TILES - 1: 2 * (S + R) // 3}.get(i, 0)
-            if split:
+        def minimum(i):
+            if i in mixed:
                 nc.vector.tensor_scalar(
-                    out=result[i][:, :split], in0=probs[i][:, :split], scalar1=inv_total[i][:], scalar2=None, op0=ALU.mult
+                    out=logits[i][:, S : S + R], in0=mixed[i], scalar1=1.0, scalar2=logits[i][:, low] if i else first_low,
+                    op0=ALU.mult, op1=ALU.min, accum_out=neg_max[i],
                 )
-            if split < S + R:
-                nc.scalar.activation(out=result[i][:, split:], in_=probs[i][:, split:], func=ACT.Copy, scale=inv_total[i][:])
+            else:
+                nc.vector.tensor_reduce(
+                    out=neg_max[i], in_=logits[i][:, S : S + R + 1], axis=mybir.AxisListType.X, op=ALU.min
+                )
+
+        def exponentials(i, columns, bias, accum):
+            if i not in probs:
+                tag = "raw3_1" if i == 0 else f"probs{i}"
+                probs[i] = keep.tile([P, S + R + PAD], F32, name=f"probs{i}", tag=tag, align_bytes=64)
+            nc.scalar.activation(
+                out=probs[i][:, columns], in_=logits[i][:, columns], func=ACT.Exp, bias=bias, scale=-1.0, accum_out=accum
+            )
+
+        def whole_row(i):
+            minimum(i)
+            exponentials(i, slice(0, S + R), neg_max[i], total[i])
+
+        def invert(i):
+            nc.vector.reciprocal(out=inv_total[i], in_=total[i])
+
+        def store(i):
             nc.sync.dma_start(out=out[i * P : (i + 1) * P, :], in_=result[i][:])
 
-        product(1)
-        fetch_scores(0)
-        for i in range(TILES):
-            if 1 <= i < TILES - 1:
-                product(i + 1)
-            mix(i)
-            if 1 <= i < TILES - 1:
-                normalise(i - 1)
-            if i + 1 < TILES:
-                fetch_scores(i + 1)
-            join(i)
-            exponentials(i)
-        normalise(TILES - 2)
-        normalise(TILES - 1)
+        def normalise_on_scalar(i, first):
+            nc.scalar.activation(
+                out=result[i][:, first:], in_=probs[i][:, first : S + R], func=ACT.Copy, scale=inv_total[i]
+            )
+
+        def product(i):
+            quantise(i, 0, PASSES)
+            for o in range(PASSES):
+                multiply(i, o)
+
+        first_low = column("first_low")
+        half_low = [column(f"half_low{n}") for n in range(2)]
+        quantise(1, 0, 1)
+        multiply(1, 0)
+        fetch_scores(0, 0)
+        fetch_scores(0, 1)
+        quantise(1, 1, 2)
+        multiply(1, 1)
+        part_one[0] = held("part_one0", "raw1_1")[0]
+        part_two[0] = held("part_two0", "grouped1")[0]
+        mix_one(0)
+        nc.vector.tensor_tensor(out=first_low, in0=half_low[0], in1=half_low[1], op=ALU.min)
+        mix_two(0)
+        fetch_scores(1)
+        mixed[0], total[0] = held("mixed0", "h_codes1")
+        join(0)
+        product(2)
+        neg_max[0] = column("neg_max0", "raw2_1")
+        whole_row(0)
+
+        part_one[1] = held("part_one1", "grouped2")[0]
+        part_two[1] = held("part_two1", "part_two1")[0]
+        mix_one(1)
+        mix_two(1)
+        inv_total[0] = column("inv_total0")
+        invert(0)
+        normalise_on_scalar(0, 0)
+        store(0)
+        fetch_scores(2)
+        mixed[1] = held("mixed1", "h_codes1")[0]
+        join(1)
+        product(3)
+        neg_max[1] = column("neg_max1")
+        total[1] = column("total1")
+        whole_row(1)
+
+        part_one[2] = held("part_one2", "part_one2")[0]
+        part_two[2] = held("part_two2", "part_two2")[0]
+        mix_one(2)
+        mix_two(2)
+        inv_total[1] = column("inv_total1")
+        invert(1)
+        normalise_on_scalar(1, 0)
+        store(1)
+        fetch_scores(3)
+        total_y = column("total_y")
+        exponentials(last, slice(0, S), logits[last][:, low], total_y)
+        mixed[2] = held("mixed2", "neg_max1")[0]
+        join(2)
+
+        part_one[3] = held("part_one3", "part_one3")[0]
+        mix_one(3)
+        part_two[3], neg_max[2] = held("part_two3", "part_two2")
+        total[2] = column("total2")
+        whole_row(2)
+        mix_two(3)
+        others = column("others")
+        nc.vector.tensor_scalar(out=others, in0=total_y, scalar1=-1.0, scalar2=None, op0=ALU.add)
+        join(3)
+        inv_total[2] = column("inv_total2")
+        invert(2)
+        neg_max[3] = column("neg_max3", "logits2")
+        minimum(3)
+        total_syn = column("total_syn")
+        exponentials(last, slice(S, S + R + 1), neg_max[last], total_syn)
+        nc.vector.tensor_scalar(
+            out=result[2][:], in0=probs[2][:, : S + R], scalar1=inv_total[2], scalar2=None, op0=ALU.mult
+        )
+        store(2)
+        total[3] = column("total3")
+        inv_total[3] = column("inv_total3")
+        factor = probs[last][:, low]
+        nc.vector.tensor_scalar(out=total[3], in0=factor, scalar1=others, scalar2=total_syn, op0=ALU.mult, op1=ALU.add)
+        invert(3)
+        nc.vector.tensor_scalar(
+            out=result[last][:, :S], in0=probs[last][:, :S], scalar1=inv_total[3], scalar2=factor,
+            op0=ALU.mult, op1=ALU.mult,
+        )
+        normalise_on_scalar(last, S)
+        rows = out[last * P :, :]
+        nc.scalar.dma_start(out=rows[:, S:], in_=result[last][:, S:])
+        nc.sync.dma_start(out=rows[:, :S], in_=result[last][:, :S])

@@ -12,6 +12,7 @@ TILES = V // P
 QUADS = 4
 SCALE_ROWS = 4
 RUN = 4
+PER = R // P
 PAD = 8
 FLOPS = 2 * K * V * S
 
@@ -40,8 +41,8 @@ def tile_picked_ymochi_soft_p_kernel(
         two_t = keep.tile([P, R // 16], U16, name="two_t")
         words = [keep.tile([P, T], I32, name=f"words{o}", align_bytes=64) for o in range(PASSES)]
         scale_rows = keep.tile([P, T], U8, name="scale_rows", align_bytes=64)
-        share_t = keep.tile([P, R // P], F32, name="share_t")
-        inv_t = keep.tile([P, R // P], F32, name="inv_t")
+        share_t = keep.tile([P, PER], F32, name="share_t")
+        inv_t = keep.tile([P, PER], F32, name="inv_t")
         raw = {(i, o): keep.tile([P, PACK, P], F32, name=f"raw{i}_{o}", align_bytes=64) for i, o in pairs}
 
         def load_words(o):
@@ -80,20 +81,19 @@ def tile_picked_ymochi_soft_p_kernel(
         for o in range(PASSES):
             nc.vector.tensor_copy(out=picked[o][:], in_=words[o][:].bitcast(U32).indirect(offs_t[:]))
 
-        per = R // P
         identity = keep.tile([P, P], F32, name="identity")
         make_identity(nc, identity[:])
-        columns_w = keep.tile([P, 2 * per], F32, name="columns_w")
-        nc.vector.tensor_tensor(out=columns_w[:, :per], in0=share_t[:], in1=inv_t[:], op=ALU.mult)
+        columns_w = keep.tile([P, 2 * PER], F32, name="columns_w")
+        nc.vector.tensor_tensor(out=columns_w[:, :PER], in0=share_t[:], in1=inv_t[:], op=ALU.mult)
         nc.vector.scalar_tensor_tensor(
-            out=columns_w[:, per:], in0=share_t[:], scalar=1.0, in1=inv_t[:], op0=ALU.subtract, op1=ALU.mult
+            out=columns_w[:, PER:], in0=share_t[:], scalar=1.0, in1=inv_t[:], op0=ALU.subtract, op1=ALU.mult
         )
-        spread = psum.tile([P, 2 * per, P], F32, name="spread")
-        for n in range(2 * per):
+        spread = psum.tile([P, 2 * PER, P], F32, name="spread")
+        for n in range(2 * PER):
             nc.tensor.transpose(spread[:, n, :], columns_w[:, n : n + 1].to_broadcast([P, P]), identity[:])
         weights = keep.tile([P, 2 * R], F32, name="weights")
         nc.scalar.copy(
-            out=weights[:].rearrange("q (t p c) -> q t p c", t=2, c=per),
+            out=weights[:].rearrange("q (t p c) -> q t p c", t=2, c=PER),
             in_=spread[:].rearrange("q (t c) p -> q t p c", t=2),
         )
         w_one = weights[:, :R]
@@ -109,26 +109,23 @@ def tile_picked_ymochi_soft_p_kernel(
             for first, end in spans[i]
         }
 
-        def interleave(copy, i, o, first, last):
+        def interleave(copy, i, o, first, end):
             copy(
-                out=grouped[i][:, o * K_PASS + PACK * first : o * K_PASS + PACK * last].rearrange(
+                out=grouped[i][:, o * K_PASS + PACK * first : o * K_PASS + PACK * end].rearrange(
                     "p (c n j) -> p c j n", n=RUN, j=PACK
                 ),
-                in_=raw[i, o][:, :, first:last].rearrange("p j (c n) -> p c j n", n=RUN),
+                in_=raw[i, o][:, :, first:end].rearrange("p j (c n) -> p c j n", n=RUN),
             )
 
-        def quantise(i, first, last):
-            tag = {(0, 0): "scales_a", (0, 1): "scales_b", (1, 0): "scales_d"}.get((i, first), "raw2_1" if i == 3 else "scales_c")
-            plane = keep.tile([P, (last - first) * P], U8, name=f"h_scales{i}_{first}", tag=tag, align_bytes=64)
-            name = f"h_codes{i}" if last == PASSES else f"early_codes{i}"
-            codes = keep.tile([P, (last - first) * P], U32, name=name, align_bytes=64)
-            for o in range(first, last):
+        def quantise(i, first, end, tag):
+            scales = keep.tile([P, (end - first) * P], U8, name=f"h_scales{i}_{first}", tag=tag, align_bytes=64)
+            name = f"h_codes{i}" if end == PASSES else f"early_codes{i}"
+            codes = keep.tile([P, (end - first) * P], U32, name=name, align_bytes=64)
+            for o in range(first, end):
                 h_codes[i, o] = codes[:, (o - first) * P : (o - first + 1) * P]
-                h_scales[i, o] = plane[:, (o - first) * P : (o - first + 1) * P]
+                h_scales[i, o] = scales[:, (o - first) * P : (o - first + 1) * P]
             nc.vector.quantize_mx(
-                out=codes[:].bitcast(FP8X4),
-                scales=plane[:],
-                in_=grouped[i][:, first * K_PASS : last * K_PASS],
+                out=codes[:].bitcast(FP8X4), scales=scales[:], in_=grouped[i][:, first * K_PASS : end * K_PASS]
             )
 
         def multiply(i, o):
@@ -143,15 +140,19 @@ def tile_picked_ymochi_soft_p_kernel(
                     stop=(o == PASSES - 1),
                 )
 
+        def product(i, first, end, tag):
+            quantise(i, first, end, tag)
+            for o in range(first, end):
+                multiply(i, o)
+
         for i, o in pairs:
             if (i, o) == (0, PASSES - 1):
                 interleave(nc.scalar.copy, i, o, 0, P // 2)
                 interleave(nc.vector.tensor_copy, i, o, P // 2, P)
             else:
                 interleave(nc.scalar.copy, i, o, 0, P)
-        for o in range(PASSES):
-            quantise(0, o, o + 1)
-            multiply(0, o)
+        product(0, 0, 1, "scales_a")
+        product(0, 1, 2, "scales_b")
 
         last = TILES - 1
         low = slice(S + R, S + R + 1)
@@ -165,20 +166,20 @@ def tile_picked_ymochi_soft_p_kernel(
         inv_total = {}
         result = [keep.tile([P, S + R], F32, name=f"result{i}") for i in range(TILES)]
 
-        def held(name, tag):
-            tile = keep.tile([P, R + PAD], F32, name=name, tag=tag, align_bytes=64)
+        def wide(name, tag=None):
+            tile = keep.tile([P, R + PAD], F32, name=name, tag=tag or name, align_bytes=64)
             return tile[:, :R], tile[:, R : R + 1]
 
         def column(name, tag=None):
             return keep.tile([P, 1], F32, name=name, tag=tag or name, align_bytes=64)[:]
 
-        def fetch_scores(i, n=0):
-            if n == 0:
+        def fetch_scores(i, half=0):
+            if half == 0:
                 logits[i] = keep.tile([P, S + R + PAD], F32, name=f"logits{i}", tag=f"logits{i % 2}", align_bytes=64)
-            first, end = spans[i][n]
+            first, end = spans[i][half]
             nc.vector.tensor_scalar(
                 out=logits[i][:, first:end], in0=banks[i, first][:], scalar1=-1.0, scalar2=None,
-                op0=ALU.mult, op1=ALU.min, accum_out=half_low[n] if i == 0 else logits[i][:, low],
+                op0=ALU.mult, op1=ALU.min, accum_out=half_low[half] if i == 0 else logits[i][:, low],
             )
 
         def mix_one(i):
@@ -187,34 +188,27 @@ def tile_picked_ymochi_soft_p_kernel(
         def mix_two(i):
             nc.vector.tensor_tensor(out=part_two[i], in0=logits[i][:].indirect(two_t[:]), in1=w_two, op=ALU.mult)
 
-        def join(i):
-            target = mixed.get(i, logits[i][:, S : S + R])
+        def join(i, target):
             nc.vector.tensor_tensor(out=target, in0=part_one[i], in1=part_two[i], op=ALU.subtract)
 
-        def minimum(i):
-            if i in mixed:
-                nc.vector.tensor_scalar(
-                    out=logits[i][:, S : S + R], in0=mixed[i], scalar1=1.0, scalar2=logits[i][:, low] if i else first_low,
-                    op0=ALU.mult, op1=ALU.min, accum_out=neg_max[i],
-                )
-            else:
-                nc.vector.tensor_reduce(
-                    out=neg_max[i], in_=logits[i][:, S : S + R + 1], axis=mybir.AxisListType.X, op=ALU.min
-                )
-
         def exponentials(i, columns, bias, accum):
-            if i not in probs:
-                tag = "raw3_1" if i == 0 else f"probs{i}"
-                probs[i] = keep.tile([P, S + R + PAD], F32, name=f"probs{i}", tag=tag, align_bytes=64)
             nc.scalar.activation(
                 out=probs[i][:, columns], in_=logits[i][:, columns], func=ACT.Exp, bias=bias, scale=-1.0, accum_out=accum
             )
 
-        def whole_row(i):
-            minimum(i)
+        def new_probs(i, tag=None):
+            probs[i] = keep.tile([P, S + R + PAD], F32, name=f"probs{i}", tag=tag or f"probs{i}", align_bytes=64)
+
+        def whole_row(i, low_y, tag=None):
+            nc.vector.tensor_scalar(
+                out=logits[i][:, S : S + R], in0=mixed[i], scalar1=1.0, scalar2=low_y,
+                op0=ALU.mult, op1=ALU.min, accum_out=neg_max[i],
+            )
+            new_probs(i, tag)
             exponentials(i, slice(0, S + R), neg_max[i], total[i])
 
         def invert(i):
+            inv_total[i] = column(f"inv_total{i}")
             nc.vector.reciprocal(out=inv_total[i], in_=total[i])
 
         def store(i):
@@ -225,90 +219,84 @@ def tile_picked_ymochi_soft_p_kernel(
                 out=result[i][:, first:], in_=probs[i][:, first : S + R], func=ACT.Copy, scale=inv_total[i]
             )
 
-        def product(i):
-            quantise(i, 0, PASSES)
-            for o in range(PASSES):
-                multiply(i, o)
-
         first_low = column("first_low")
-        half_low = [column(f"half_low{n}") for n in range(2)]
-        quantise(1, 0, 1)
-        multiply(1, 0)
+        half_low = [column(f"half_low{half}") for half in range(len(spans[0]))]
+        product(1, 0, 1, "scales_d")
         fetch_scores(0, 0)
         fetch_scores(0, 1)
-        quantise(1, 1, 2)
-        multiply(1, 1)
-        part_one[0] = held("part_one0", "raw1_1")[0]
-        part_two[0] = held("part_two0", "grouped1")[0]
+        product(1, 1, 2, "scales_c")
+        part_one[0] = wide("part_one0", "raw1_1")[0]
+        part_two[0] = wide("part_two0", "grouped1")[0]
         mix_one(0)
         nc.vector.tensor_tensor(out=first_low, in0=half_low[0], in1=half_low[1], op=ALU.min)
         mix_two(0)
         fetch_scores(1)
-        mixed[0], total[0] = held("mixed0", "h_codes1")
-        join(0)
-        product(2)
+        mixed[0], total[0] = wide("mixed0", "h_codes1")
+        join(0, mixed[0])
+        product(2, 0, PASSES, "scales_c")
         neg_max[0] = column("neg_max0", "raw2_1")
-        whole_row(0)
+        whole_row(0, first_low, "raw3_1")
 
-        part_one[1] = held("part_one1", "grouped2")[0]
-        part_two[1] = held("part_two1", "part_two1")[0]
+        part_one[1] = wide("part_one1", "grouped2")[0]
+        part_two[1] = wide("part_two1")[0]
         mix_one(1)
         mix_two(1)
-        inv_total[0] = column("inv_total0")
         invert(0)
         normalise_on_scalar(0, 0)
         store(0)
         fetch_scores(2)
-        mixed[1] = held("mixed1", "h_codes1")[0]
-        join(1)
-        product(3)
+        mixed[1] = wide("mixed1", "h_codes1")[0]
+        join(1, mixed[1])
+        product(3, 0, PASSES, "raw2_1")
         neg_max[1] = column("neg_max1")
         total[1] = column("total1")
-        whole_row(1)
+        whole_row(1, logits[1][:, low])
 
-        part_one[2] = held("part_one2", "part_one2")[0]
-        part_two[2] = held("part_two2", "part_two2")[0]
+        part_one[2] = wide("part_one2")[0]
+        part_two[2] = wide("part_two2")[0]
         mix_one(2)
         mix_two(2)
-        inv_total[1] = column("inv_total1")
         invert(1)
         normalise_on_scalar(1, 0)
         store(1)
-        fetch_scores(3)
+        fetch_scores(last)
         total_y = column("total_y")
+        new_probs(last)
         exponentials(last, slice(0, S), logits[last][:, low], total_y)
-        mixed[2] = held("mixed2", "neg_max1")[0]
-        join(2)
+        mixed[2] = wide("mixed2", "neg_max1")[0]
+        join(2, mixed[2])
 
-        part_one[3] = held("part_one3", "part_one3")[0]
-        mix_one(3)
-        part_two[3], neg_max[2] = held("part_two3", "part_two2")
+        part_one[last] = wide("part_one3")[0]
+        mix_one(last)
+        part_two[last], neg_max[2] = wide("part_two3", "part_two2")
         total[2] = column("total2")
-        whole_row(2)
-        mix_two(3)
-        others = column("others")
-        nc.vector.tensor_scalar(out=others, in0=total_y, scalar1=-1.0, scalar2=None, op0=ALU.add)
-        join(3)
-        inv_total[2] = column("inv_total2")
+        whole_row(2, logits[2][:, low])
+        mix_two(last)
+        total_y_less_one = column("others")
+        nc.vector.tensor_scalar(out=total_y_less_one, in0=total_y, scalar1=-1.0, scalar2=None, op0=ALU.add)
+        join(last, logits[last][:, S : S + R])
         invert(2)
-        neg_max[3] = column("neg_max3", "logits2")
-        minimum(3)
-        total_syn = column("total_syn")
-        exponentials(last, slice(S, S + R + 1), neg_max[last], total_syn)
+        syn_and_low = slice(S, S + R + 1)
+        neg_max[last] = column("neg_max3")
+        nc.vector.tensor_reduce(
+            out=neg_max[last], in_=logits[last][:, syn_and_low], axis=mybir.AxisListType.X, op=ALU.min
+        )
+        total_syn_and_factor = column("total_syn")
+        exponentials(last, syn_and_low, neg_max[last], total_syn_and_factor)
         nc.vector.tensor_scalar(
             out=result[2][:], in0=probs[2][:, : S + R], scalar1=inv_total[2], scalar2=None, op0=ALU.mult
         )
         store(2)
-        total[3] = column("total3")
-        inv_total[3] = column("inv_total3")
         factor = probs[last][:, low]
-        nc.vector.tensor_scalar(out=total[3], in0=factor, scalar1=others, scalar2=total_syn, op0=ALU.mult, op1=ALU.add)
-        invert(3)
+        total[last] = column("total3")
         nc.vector.tensor_scalar(
-            out=result[last][:, :S], in0=probs[last][:, :S], scalar1=inv_total[3], scalar2=factor,
+            out=total[last], in0=factor, scalar1=total_y_less_one, scalar2=total_syn_and_factor,
+            op0=ALU.mult, op1=ALU.add,
+        )
+        invert(last)
+        nc.vector.tensor_scalar(
+            out=result[last][:, :S], in0=probs[last][:, :S], scalar1=inv_total[last], scalar2=factor,
             op0=ALU.mult, op1=ALU.mult,
         )
         normalise_on_scalar(last, S)
-        rows = out[last * P :, :]
-        nc.scalar.dma_start(out=rows[:, S:], in_=result[last][:, S:])
-        nc.sync.dma_start(out=rows[:, :S], in_=result[last][:, :S])
+        store(last)

@@ -42,7 +42,7 @@ def tile_picked_ymochi_soft_p_kernel(
         words = [keep.tile([P, T], I32, name=f"words{o}", align_bytes=64) for o in range(PASSES)]
         scale_rows = keep.tile([P, T], U8, name="scale_rows", align_bytes=64)
         share_t = keep.tile([P, PER], F32, name="share_t")
-        inv_t = keep.tile([P, PER], F32, name="inv_t")
+        inv_t = keep.tile([P, PER], F32, name="inv_t", align_bytes=64)
         raw = {(i, o): keep.tile([P, PACK, P], F32, name=f"raw{i}_{o}", align_bytes=64) for i, o in pairs}
 
         def load_words(o):
@@ -60,10 +60,10 @@ def tile_picked_ymochi_soft_p_kernel(
                 in_=x_scales[:, SCALE_ROWS * quad : SCALE_ROWS * (quad + 1), :].bitcast(I32),
             )
         nc.sync.dma_start(out=offs_t[:], in_=offs)
+        load_words(0)
         for tile, rows in ((share_t, share), (inv_t, inv)):
             nc.sync.dma_start(out=tile[:], in_=rows[0, :].rearrange("(p c) -> p c", p=P))
-        for o in range(PASSES):
-            load_words(o)
+        load_words(1)
         for o in range(PASSES):
             load_queries(0, o)
         nc.sync.dma_start(out=one_t[:], in_=one)
@@ -71,15 +71,6 @@ def tile_picked_ymochi_soft_p_kernel(
         for i in range(1, TILES):
             for o in range(PASSES):
                 load_queries(i, o)
-
-        picked_scales = keep.tile([P, S], U8, name="picked_scales", align_bytes=64)
-        picked = [keep.tile([P, S], U32, name=f"picked{o}", align_bytes=64) for o in range(PASSES)]
-        nc.vector.memset(scale_rows[:].bitcast(I32), 0)
-        for quad in range(QUADS):
-            nc.vector.tensor_copy(out=scale_rows[live[quad], :].bitcast(I32), in_=landed_rows[live[quad], :].bitcast(I32))
-        nc.vector.tensor_copy(out=picked_scales[:], in_=scale_rows[:].indirect(offs_t[:]))
-        for o in range(PASSES):
-            nc.vector.tensor_copy(out=picked[o][:], in_=words[o][:].bitcast(U32).indirect(offs_t[:]))
 
         identity = keep.tile([P, P], F32, name="identity")
         make_identity(nc, identity[:])
@@ -98,6 +89,18 @@ def tile_picked_ymochi_soft_p_kernel(
         )
         w_one = weights[:, :R]
         w_two = weights[:, R:]
+
+        picked_scales = keep.tile([P, S], U8, name="picked_scales", align_bytes=64)
+        picked = [
+            keep.tile([P, S], U32, name=f"picked{o}", tag=tag, align_bytes=64)
+            for o, tag in enumerate(("inv_t", "picked1"))
+        ]
+        nc.vector.memset(scale_rows[:].bitcast(I32), 0)
+        for quad in range(QUADS):
+            nc.vector.tensor_copy(out=scale_rows[live[quad], :].bitcast(I32), in_=landed_rows[live[quad], :].bitcast(I32))
+        nc.vector.tensor_copy(out=picked_scales[:], in_=scale_rows[:].indirect(offs_t[:]))
+        for o in range(PASSES):
+            nc.vector.tensor_copy(out=picked[o][:], in_=words[o][:].bitcast(U32).indirect(offs_t[:]))
 
         grouped = [keep.tile([P, PASSES * K_PASS], BF16, name=f"grouped{i}", align_bytes=64) for i in range(TILES)]
         h_codes = {}
@@ -263,6 +266,7 @@ def tile_picked_ymochi_soft_p_kernel(
         total_y = column("total_y")
         new_probs(last)
         exponentials(last, slice(0, S), logits[last][:, low], total_y)
+        total_y_less_one = column("others")
         mixed[2] = wide("mixed2", "neg_max1")[0]
         join(2, mixed[2])
 
@@ -271,9 +275,8 @@ def tile_picked_ymochi_soft_p_kernel(
         part_two[last], neg_max[2] = wide("part_two3", "part_two2")
         total[2] = column("total2")
         whole_row(2, logits[2][:, low])
+        nc.scalar.activation(out=total_y_less_one, in_=total_y, func=ACT.Copy, bias=-1.0)
         mix_two(last)
-        total_y_less_one = column("others")
-        nc.vector.tensor_scalar(out=total_y_less_one, in0=total_y, scalar1=-1.0, scalar2=None, op0=ALU.add)
         join(last, logits[last][:, S : S + R])
         invert(2)
         syn_and_low = slice(S, S + R + 1)
@@ -289,9 +292,8 @@ def tile_picked_ymochi_soft_p_kernel(
         store(2)
         factor = probs[last][:, low]
         total[last] = column("total3")
-        nc.vector.tensor_scalar(
-            out=total[last], in0=factor, scalar1=total_y_less_one, scalar2=total_syn_and_factor,
-            op0=ALU.mult, op1=ALU.add,
+        nc.scalar.activation(
+            out=total[last], in_=factor, func=ACT.Identity, scale=total_y_less_one, bias=total_syn_and_factor
         )
         invert(last)
         nc.vector.tensor_scalar(

@@ -48,9 +48,9 @@ def tile_picked_ymochi_soft_p_kernel(
         def load_words(o):
             nc.sync.dma_start(out=words[o][:], in_=x_words[o].rearrange("p n t -> p (n t)").bitcast(I32))
 
-        def load_queries(i, o):
+        def load_queries(i, o, queue=nc.sync):
             rows = hT[o * K_PASS : (o + 1) * K_PASS, i * P : (i + 1) * P]
-            nc.sync.dma_start(out=raw[i, o][:], in_=rows.rearrange("(p j) q -> p j q", j=PACK))
+            queue.dma_start(out=raw[i, o][:], in_=rows.rearrange("(p j) q -> p j q", j=PACK))
 
         landed_rows = keep.tile([P, T], U8, name="landed_rows", align_bytes=64)
         live = [slice(32 * quad, 32 * quad + SCALE_ROWS * PASSES) for quad in range(QUADS)]
@@ -62,12 +62,12 @@ def tile_picked_ymochi_soft_p_kernel(
         nc.sync.dma_start(out=offs_t[:], in_=offs)
         load_words(0)
         for tile, rows in ((share_t, share), (inv_t, inv)):
-            nc.sync.dma_start(out=tile[:], in_=rows[0, :].rearrange("(p c) -> p c", p=P))
-        load_words(1)
+            nc.scalar.dma_start(out=tile[:], in_=rows[0, :].rearrange("(p c) -> p c", p=P))
         for o in range(PASSES):
-            load_queries(0, o)
+            load_queries(0, o, nc.scalar)
         nc.sync.dma_start(out=one_t[:], in_=one)
         nc.sync.dma_start(out=two_t[:], in_=two)
+        load_words(1)
         for i in range(1, TILES):
             for o in range(PASSES):
                 load_queries(i, o)
@@ -91,16 +91,21 @@ def tile_picked_ymochi_soft_p_kernel(
         w_two = weights[:, R:]
 
         picked_scales = keep.tile([P, S], U8, name="picked_scales", align_bytes=64)
-        picked = [
-            keep.tile([P, S], U32, name=f"picked{o}", tag=tag, align_bytes=64)
-            for o, tag in enumerate(("inv_t", "picked1"))
-        ]
+        picked = {}
         nc.vector.memset(scale_rows[:].bitcast(I32), 0)
         for quad in range(QUADS):
             nc.vector.tensor_copy(out=scale_rows[live[quad], :].bitcast(I32), in_=landed_rows[live[quad], :].bitcast(I32))
         nc.vector.tensor_copy(out=picked_scales[:], in_=scale_rows[:].indirect(offs_t[:]))
-        for o in range(PASSES):
-            nc.vector.tensor_copy(out=picked[o][:], in_=words[o][:].bitcast(U32).indirect(offs_t[:]))
+
+        def pick_words(o, pieces, tag):
+            picked[o] = keep.tile([P, S], U32, name=f"picked{o}", tag=tag, align_bytes=64)
+            for first, end in pieces:
+                nc.vector.tensor_copy(
+                    out=picked[o][:, first:end],
+                    in_=words[o][:].bitcast(U32).indirect(offs_t[:, first // 16 : end // 16]),
+                )
+
+        pick_words(0, [(0, S)], "picked0")
 
         grouped = [keep.tile([P, PASSES * K_PASS], BF16, name=f"grouped{i}", align_bytes=64) for i in range(TILES)]
         h_codes = {}
@@ -149,13 +154,11 @@ def tile_picked_ymochi_soft_p_kernel(
                 multiply(i, o)
 
         for i, o in pairs:
-            if (i, o) == (0, PASSES - 1):
-                interleave(nc.scalar.copy, i, o, 0, P // 2)
-                interleave(nc.vector.tensor_copy, i, o, P // 2, P)
-            else:
-                interleave(nc.scalar.copy, i, o, 0, P)
+            interleave(nc.scalar.copy, i, o, 0, P)
         product(0, 0, 1, "scales_a")
-        product(0, 1, 2, "scales_b")
+        quantise(0, 1, 2, "scales_b")
+        pick_words(1, spans[0], "grouped0")
+        multiply(0, 1)
 
         last = TILES - 1
         low = slice(S + R, S + R + 1)
@@ -178,7 +181,7 @@ def tile_picked_ymochi_soft_p_kernel(
 
         def fetch_scores(i, half=0):
             if half == 0:
-                logits[i] = keep.tile([P, S + R + PAD], F32, name=f"logits{i}", tag=f"logits{i % 2}", align_bytes=64)
+                logits[i] = keep.tile([P, S + R + PAD], F32, name=f"logits{i}", tag=("raw1_0", "half_low0")[i % 2], align_bytes=64)
             first, end = spans[i][half]
             nc.vector.tensor_scalar(
                 out=logits[i][:, first:end], in0=banks[i, first][:], scalar1=-1.0, scalar2=None,
@@ -224,10 +227,10 @@ def tile_picked_ymochi_soft_p_kernel(
 
         first_low = column("first_low")
         half_low = [column(f"half_low{half}") for half in range(len(spans[0]))]
-        product(1, 0, 1, "scales_d")
         fetch_scores(0, 0)
+        product(1, 0, 1, "scales_d")
         fetch_scores(0, 1)
-        product(1, 1, 2, "scales_c")
+        product(1, 1, 2, "scales_b")
         part_one[0] = wide("part_one0", "raw1_1")[0]
         part_two[0] = wide("part_two0", "grouped1")[0]
         mix_one(0)
@@ -236,7 +239,7 @@ def tile_picked_ymochi_soft_p_kernel(
         fetch_scores(1)
         mixed[0], total[0] = wide("mixed0", "h_codes1")
         join(0, mixed[0])
-        product(2, 0, PASSES, "scales_c")
+        product(2, 0, PASSES, "scales_b")
         neg_max[0] = column("neg_max0", "raw2_1")
         whole_row(0, first_low, "raw3_1")
 

@@ -65,9 +65,9 @@ def tile_picked_ymochi_soft_p_kernel(
             nc.scalar.dma_start(out=tile[:], in_=rows[0, :].rearrange("(p c) -> p c", p=P))
         for o in range(PASSES):
             load_queries(0, o, nc.scalar)
+        load_words(1)
         nc.sync.dma_start(out=one_t[:], in_=one)
         nc.sync.dma_start(out=two_t[:], in_=two)
-        load_words(1)
         for i in range(1, TILES):
             for o in range(PASSES):
                 load_queries(i, o)

@@ -153,7 +153,7 @@ def tile_picked_ymochi_soft_p_kernel(
             for o in range(first, end):
                 multiply(i, o)
 
-        for i, o in pairs:
+        for i, o in pairs[: (TILES - 1) * PASSES]:
             interleave(nc.scalar.copy, i, o, 0, P)
         product(0, 0, 1, "scales_a")
         quantise(0, 1, 2, "scales_b")
@@ -163,39 +163,63 @@ def tile_picked_ymochi_soft_p_kernel(
         last = TILES - 1
         low = slice(S + R, S + R + 1)
         logits = {}
-        part_one = {}
-        part_two = {}
-        mixed = {}
+        parts = {}
         probs = {}
         neg_max = {}
         total = {}
         inv_total = {}
         result = [keep.tile([P, S + R], F32, name=f"result{i}") for i in range(TILES)]
 
-        def wide(name, tag=None):
-            tile = keep.tile([P, R + PAD], F32, name=name, tag=tag or name, align_bytes=64)
-            return tile[:, :R], tile[:, R : R + 1]
-
         def column(name, tag=None):
             return keep.tile([P, 1], F32, name=name, tag=tag or name, align_bytes=64)[:]
 
-        def fetch_scores(i, half=0):
+        def fetch_scores(i, low_y, half=0, tag=None):
             if half == 0:
-                logits[i] = keep.tile([P, S + R + PAD], F32, name=f"logits{i}", tag=("raw1_0", "half_low0")[i % 2], align_bytes=64)
+                logits[i] = keep.tile([P, S + R + PAD], F32, name=f"logits{i}", tag=tag or f"logits{i}", align_bytes=64)
             first, end = spans[i][half]
             nc.vector.tensor_scalar(
                 out=logits[i][:, first:end], in0=banks[i, first][:], scalar1=-1.0, scalar2=None,
-                op0=ALU.mult, op1=ALU.min, accum_out=half_low[half] if i == 0 else logits[i][:, low],
+                op0=ALU.mult, op1=ALU.min, accum_out=logits[i][:, low] if low_y is None else low_y,
             )
 
-        def mix_one(i):
-            nc.vector.tensor_tensor(out=part_one[i], in0=logits[i][:].indirect(one_t[:]), in1=w_one, op=ALU.mult)
+        def wide(name, columns, tag=None):
+            return keep.tile([P, columns], F32, name=name, tag=tag or name, align_bytes=64)
 
-        def mix_two(i):
-            nc.vector.tensor_tensor(out=part_two[i], in0=logits[i][:].indirect(two_t[:]), in1=w_two, op=ALU.mult)
+        def mix(i, n, tag=None):
+            parts[i, n] = wide(f"part{i}_{n}", R, tag)[:]
+            nc.vector.tensor_tensor(
+                out=parts[i, n], in0=logits[i][:].indirect((one_t, two_t)[n][:]), in1=(w_one, w_two)[n], op=ALU.mult
+            )
 
-        def join(i, target):
-            nc.vector.tensor_tensor(out=target, in0=part_one[i], in1=part_two[i], op=ALU.subtract)
+        fetched = {}
+
+        def gather(i, n, tag=None):
+            if i not in fetched:
+                fetched[i] = wide(f"fetched{i}", 2 * R, tag)
+            nc.scalar.activation(
+                out=fetched[i][:, n * R : (n + 1) * R], in_=logits[i][:].indirect((one_t, two_t)[n][:]), func=ACT.Copy
+            )
+
+        def weigh(i, tag=None, first=0):
+            weighed = wide(f"weighed{i}", 2 * R, tag)
+            nc.vector.tensor_tensor(
+                out=weighed[:, first * R :], in0=fetched[i][:, first * R :], in1=weights[:, first * R :], op=ALU.mult
+            )
+            for n in range(first, 2):
+                parts[i, n] = weighed[:, n * R : (n + 1) * R]
+
+        mixed = {}
+
+        def join(i, tag=None):
+            mixed[i] = logits[i][:, S : S + R] if i == last else wide(f"mixed{i}", R, tag)[:]
+            nc.vector.tensor_tensor(out=mixed[i], in0=parts[i, 0], in1=parts[i, 1], op=ALU.subtract)
+
+        def minimum(i, low_y, tag=None):
+            neg_max[i] = column(f"neg_max{i}", tag)
+            nc.vector.tensor_scalar(
+                out=logits[i][:, S : S + R], in0=mixed[i], scalar1=1.0, scalar2=low_y,
+                op0=ALU.mult, op1=ALU.min, accum_out=neg_max[i],
+            )
 
         def exponentials(i, columns, bias, accum):
             nc.scalar.activation(
@@ -203,14 +227,11 @@ def tile_picked_ymochi_soft_p_kernel(
             )
 
         def new_probs(i, tag=None):
-            probs[i] = keep.tile([P, S + R + PAD], F32, name=f"probs{i}", tag=tag or f"probs{i}", align_bytes=64)
+            probs[i] = wide(f"probs{i}", S + R + PAD, tag)
 
-        def whole_row(i, low_y, tag=None):
-            nc.vector.tensor_scalar(
-                out=logits[i][:, S : S + R], in0=mixed[i], scalar1=1.0, scalar2=low_y,
-                op0=ALU.mult, op1=ALU.min, accum_out=neg_max[i],
-            )
+        def whole_row(i, tag=None):
             new_probs(i, tag)
+            total[i] = column(f"total{i}")
             exponentials(i, slice(0, S + R), neg_max[i], total[i])
 
         def invert(i):
@@ -225,73 +246,67 @@ def tile_picked_ymochi_soft_p_kernel(
                 out=result[i][:, first:], in_=probs[i][:, first : S + R], func=ACT.Copy, scale=inv_total[i]
             )
 
-        first_low = column("first_low")
+        def normalise_on_vector(i):
+            nc.vector.tensor_scalar(
+                out=result[i][:], in0=probs[i][:, : S + R], scalar1=inv_total[i], scalar2=None, op0=ALU.mult
+            )
+
         half_low = [column(f"half_low{half}") for half in range(len(spans[0]))]
-        fetch_scores(0, 0)
+        low_y = [column(f"low_y{i}") for i in range(last)]
+        fetch_scores(0, half_low[0], 0, "raw1_0")
         product(1, 0, 1, "scales_d")
-        fetch_scores(0, 1)
+        fetch_scores(0, half_low[1], 1)
         product(1, 1, 2, "scales_b")
-        part_one[0] = wide("part_one0", "raw1_1")[0]
-        part_two[0] = wide("part_two0", "grouped1")[0]
-        mix_one(0)
-        nc.vector.tensor_tensor(out=first_low, in0=half_low[0], in1=half_low[1], op=ALU.min)
-        mix_two(0)
-        fetch_scores(1)
-        mixed[0], total[0] = wide("mixed0", "h_codes1")
-        join(0, mixed[0])
-        product(2, 0, PASSES, "scales_b")
-        neg_max[0] = column("neg_max0", "raw2_1")
-        whole_row(0, first_low, "raw3_1")
-
-        part_one[1] = wide("part_one1", "grouped2")[0]
-        part_two[1] = wide("part_two1")[0]
-        mix_one(1)
-        mix_two(1)
+        mix(0, 0, "raw1_1")
+        nc.vector.tensor_tensor(out=low_y[0], in0=half_low[0], in1=half_low[1], op=ALU.min)
+        gather(0, 1, "raw2_0")
+        for o in range(PASSES):
+            interleave(nc.scalar.copy, last, o, 0, P)
+        product(2, 0, PASSES, "scales_2")
+        weigh(0, "raw2_1", 1)
+        fetch_scores(1, low_y[1])
+        join(0, "h_codes1")
+        product(3, 0, PASSES, "grouped2")
+        gather(1, 0, "raw3_0")
+        gather(1, 1)
+        minimum(0, low_y[0], "raw3_1")
+        whole_row(0)
+        fetch_scores(2, low_y[2], 0, "grouped3")
+        weigh(1, "h_codes1")
         invert(0)
-        normalise_on_scalar(0, 0)
+        join(1, "raw3_1")
+        normalise_on_vector(0)
         store(0)
-        fetch_scores(2)
-        mixed[1] = wide("mixed1", "h_codes1")[0]
-        join(1, mixed[1])
-        product(3, 0, PASSES, "raw2_1")
-        neg_max[1] = column("neg_max1")
-        total[1] = column("total1")
-        whole_row(1, logits[1][:, low])
-
-        part_one[2] = wide("part_one2")[0]
-        part_two[2] = wide("part_two2")[0]
-        mix_one(2)
-        mix_two(2)
+        gather(2, 0, "low_y0")
+        gather(2, 1)
+        minimum(1, low_y[1])
+        whole_row(1)
+        fetch_scores(3, None, 0, "h_codes1")
+        weigh(2, "raw3_1")
         invert(1)
-        normalise_on_scalar(1, 0)
-        store(1)
-        fetch_scores(last)
+        gather(3, 1, "low_y1")
         total_y = column("total_y")
         new_probs(last)
         exponentials(last, slice(0, S), logits[last][:, low], total_y)
+        normalise_on_scalar(1, 0)
+        store(1)
+        mix(3, 0)
+        join(2, "neg_max1")
+        weigh(3, "raw3_1", 1)
+        minimum(2, low_y[2])
         total_y_less_one = column("others")
-        mixed[2] = wide("mixed2", "neg_max1")[0]
-        join(2, mixed[2])
-
-        part_one[last] = wide("part_one3")[0]
-        mix_one(last)
-        part_two[last], neg_max[2] = wide("part_two3", "part_two2")
-        total[2] = column("total2")
-        whole_row(2, logits[2][:, low])
+        whole_row(2)
         nc.scalar.activation(out=total_y_less_one, in_=total_y, func=ACT.Copy, bias=-1.0)
-        mix_two(last)
-        join(last, logits[last][:, S : S + R])
-        invert(2)
-        syn_and_low = slice(S, S + R + 1)
+        join(3)
         neg_max[last] = column("neg_max3")
         nc.vector.tensor_reduce(
-            out=neg_max[last], in_=logits[last][:, syn_and_low], axis=mybir.AxisListType.X, op=ALU.min
+            out=neg_max[last], in_=logits[last][:, S : S + R + 1], axis=mybir.AxisListType.X, op=ALU.min
         )
+        syn_and_low = slice(S, S + R + 1)
         total_syn_and_factor = column("total_syn")
         exponentials(last, syn_and_low, neg_max[last], total_syn_and_factor)
-        nc.vector.tensor_scalar(
-            out=result[2][:], in0=probs[2][:, : S + R], scalar1=inv_total[2], scalar2=None, op0=ALU.mult
-        )
+        invert(2)
+        normalise_on_vector(2)
         store(2)
         factor = probs[last][:, low]
         total[last] = column("total3")

@@ -153,7 +153,7 @@ def tile_picked_ymochi_soft_p_kernel(
             for o in range(first, end):
                 multiply(i, o)
 
-        for i, o in pairs[: (TILES - 1) * PASSES]:
+        for i, o in pairs:
             interleave(nc.scalar.copy, i, o, 0, P)
         product(0, 0, 1, "scales_a")
         quantise(0, 1, 2, "scales_b")
@@ -168,7 +168,7 @@ def tile_picked_ymochi_soft_p_kernel(
         neg_max = {}
         total = {}
         inv_total = {}
-        result = [keep.tile([P, S + R], F32, name=f"result{i}") for i in range(TILES)]
+        result = {}
 
         def column(name, tag=None):
             return keep.tile([P, 1], F32, name=name, tag=tag or name, align_bytes=64)[:]
@@ -203,7 +203,10 @@ def tile_picked_ymochi_soft_p_kernel(
         def weigh(i, tag=None, first=0):
             weighed = wide(f"weighed{i}", 2 * R, tag)
             nc.vector.tensor_tensor(
-                out=weighed[:, first * R :], in0=fetched[i][:, first * R :], in1=weights[:, first * R :], op=ALU.mult
+                out=weighed[:, first * R :].rearrange("q (t p c) -> q t p c", p=P, c=PER),
+                in0=fetched[i][:, first * R :].rearrange("q (t p c) -> q t p c", p=P, c=PER),
+                in1=spread[:, first * PER :, :].rearrange("q (t c) p -> q t p c", c=PER),
+                op=ALU.mult,
             )
             for n in range(first, 2):
                 parts[i, n] = weighed[:, n * R : (n + 1) * R]
@@ -241,6 +244,14 @@ def tile_picked_ymochi_soft_p_kernel(
         def store(i):
             nc.sync.dma_start(out=out[i * P : (i + 1) * P, :], in_=result[i][:])
 
+        def new_result(i, tag=None):
+            result[i] = wide(f"result{i}", S + R, tag)
+
+        def normalise_on_gpsimd(i):
+            nc.gpsimd.tensor_scalar(
+                out=result[i][:], in0=probs[i][:, : S + R], scalar1=inv_total[i], scalar2=0.0, op0=ALU.mult, op1=ALU.add
+            )
+
         def normalise_on_scalar(i, first):
             nc.scalar.activation(
                 out=result[i][:, first:], in_=probs[i][:, first : S + R], func=ACT.Copy, scale=inv_total[i]
@@ -259,40 +270,39 @@ def tile_picked_ymochi_soft_p_kernel(
         product(1, 1, 2, "scales_b")
         mix(0, 0, "raw1_1")
         nc.vector.tensor_tensor(out=low_y[0], in0=half_low[0], in1=half_low[1], op=ALU.min)
-        gather(0, 1, "raw2_0")
-        for o in range(PASSES):
-            interleave(nc.scalar.copy, last, o, 0, P)
-        product(2, 0, PASSES, "scales_2")
-        weigh(0, "raw2_1", 1)
+        mix(0, 1, "grouped1")
         fetch_scores(1, low_y[1])
-        join(0, "h_codes1")
-        product(3, 0, PASSES, "grouped2")
-        gather(1, 0, "raw3_0")
-        gather(1, 1)
-        minimum(0, low_y[0], "raw3_1")
+        product(2, 0, PASSES, "scales_b")
+        join(0, "raw2_1")
+        mix(1, 0, "grouped2")
+        minimum(0, low_y[0])
+        product(3, 0, PASSES, "raw1_1")
+        gather(1, 1, "raw3_0")
         whole_row(0)
-        fetch_scores(2, low_y[2], 0, "grouped3")
-        weigh(1, "h_codes1")
+        fetch_scores(2, low_y[2], 0, "raw3_1")
+        weigh(1, "raw2_1", 1)
         invert(0)
-        join(1, "raw3_1")
-        normalise_on_vector(0)
+        join(1, "neg_max0")
+        new_result(0, "raw2_1")
+        normalise_on_gpsimd(0)
         store(0)
-        gather(2, 0, "low_y0")
+        gather(2, 0)
         gather(2, 1)
+        fetch_scores(3, None, 0, "raw1_0")
         minimum(1, low_y[1])
+        gather(3, 1)
         whole_row(1)
-        fetch_scores(3, None, 0, "h_codes1")
-        weigh(2, "raw3_1")
-        invert(1)
-        gather(3, 1, "low_y1")
         total_y = column("total_y")
-        new_probs(last)
+        new_probs(last, "low_y1")
         exponentials(last, slice(0, S), logits[last][:, low], total_y)
-        normalise_on_scalar(1, 0)
-        store(1)
+        weigh(2, "grouped2")
         mix(3, 0)
-        join(2, "neg_max1")
-        weigh(3, "raw3_1", 1)
+        join(2)
+        invert(1)
+        new_result(1, "grouped2")
+        normalise_on_gpsimd(1)
+        store(1)
+        weigh(3, "neg_max1", 1)
         minimum(2, low_y[2])
         total_y_less_one = column("others")
         whole_row(2)
@@ -306,6 +316,7 @@ def tile_picked_ymochi_soft_p_kernel(
         total_syn_and_factor = column("total_syn")
         exponentials(last, syn_and_low, neg_max[last], total_syn_and_factor)
         invert(2)
+        new_result(2)
         normalise_on_vector(2)
         store(2)
         factor = probs[last][:, low]
@@ -314,6 +325,7 @@ def tile_picked_ymochi_soft_p_kernel(
             out=total[last], in_=factor, func=ACT.Identity, scale=total_y_less_one, bias=total_syn_and_factor
         )
         invert(last)
+        new_result(last)
         nc.vector.tensor_scalar(
             out=result[last][:, :S], in0=probs[last][:, :S], scalar1=inv_total[last], scalar2=factor,
             op0=ALU.mult, op1=ALU.mult,

@@ -173,13 +173,13 @@ def tile_picked_ymochi_soft_p_kernel(
         def column(name, tag=None):
             return keep.tile([P, 1], F32, name=name, tag=tag or name, align_bytes=64)[:]
 
-        def fetch_scores(i, low_y, half=0, tag=None):
+        def fetch_scores(i, half=0, tag=None):
             if half == 0:
                 logits[i] = keep.tile([P, S + R + PAD], F32, name=f"logits{i}", tag=tag or f"logits{i}", align_bytes=64)
             first, end = spans[i][half]
             nc.vector.tensor_scalar(
                 out=logits[i][:, first:end], in0=banks[i, first][:], scalar1=-1.0, scalar2=None,
-                op0=ALU.mult, op1=ALU.min, accum_out=logits[i][:, low] if low_y is None else low_y,
+                op0=ALU.mult, op1=ALU.min, accum_out=logits[i][:, S + R + half : S + R + half + 1],
             )
 
         def wide(name, columns, tag=None):
@@ -211,17 +211,13 @@ def tile_picked_ymochi_soft_p_kernel(
             for n in range(first, 2):
                 parts[i, n] = weighed[:, n * R : (n + 1) * R]
 
-        mixed = {}
+        def join(i):
+            nc.vector.tensor_tensor(out=logits[i][:, S : S + R], in0=parts[i, 0], in1=parts[i, 1], op=ALU.subtract)
 
-        def join(i, tag=None):
-            mixed[i] = logits[i][:, S : S + R] if i == last else wide(f"mixed{i}", R, tag)[:]
-            nc.vector.tensor_tensor(out=mixed[i], in0=parts[i, 0], in1=parts[i, 1], op=ALU.subtract)
-
-        def minimum(i, low_y, tag=None):
+        def minimum(i, tag=None):
             neg_max[i] = column(f"neg_max{i}", tag)
-            nc.vector.tensor_scalar(
-                out=logits[i][:, S : S + R], in0=mixed[i], scalar1=1.0, scalar2=low_y,
-                op0=ALU.mult, op1=ALU.min, accum_out=neg_max[i],
+            nc.vector.tensor_reduce(
+                out=neg_max[i], in_=logits[i][:, S : S + R + len(spans[i])], axis=mybir.AxisListType.X, op=ALU.min
             )
 
         def exponentials(i, columns, bias, accum):
@@ -247,9 +243,9 @@ def tile_picked_ymochi_soft_p_kernel(
         def new_result(i, tag=None):
             result[i] = wide(f"result{i}", S + R, tag)
 
-        def normalise_on_gpsimd(i):
+        def normalise_on_gpsimd(i, end=S + R):
             nc.gpsimd.tensor_scalar(
-                out=result[i][:], in0=probs[i][:, : S + R], scalar1=inv_total[i], scalar2=0.0, op0=ALU.mult, op1=ALU.add
+                out=result[i][:, :end], in0=probs[i][:, :end], scalar1=inv_total[i], scalar2=0.0, op0=ALU.mult, op1=ALU.add
             )
 
         def normalise_on_scalar(i, first):
@@ -262,56 +258,51 @@ def tile_picked_ymochi_soft_p_kernel(
                 out=result[i][:], in0=probs[i][:, : S + R], scalar1=inv_total[i], scalar2=None, op0=ALU.mult
             )
 
-        half_low = [column(f"half_low{half}") for half in range(len(spans[0]))]
-        low_y = [column(f"low_y{i}") for i in range(last)]
-        fetch_scores(0, half_low[0], 0, "raw1_0")
+        fetch_scores(0, 0, "raw1_0")
         product(1, 0, 1, "scales_d")
-        fetch_scores(0, half_low[1], 1)
+        fetch_scores(0, 1)
         product(1, 1, 2, "scales_b")
         mix(0, 0, "raw1_1")
-        nc.vector.tensor_tensor(out=low_y[0], in0=half_low[0], in1=half_low[1], op=ALU.min)
         mix(0, 1, "grouped1")
-        fetch_scores(1, low_y[1])
+        fetch_scores(1)
+        join(0)
         product(2, 0, PASSES, "scales_b")
-        join(0, "raw2_1")
+        minimum(0)
         mix(1, 0, "grouped2")
-        minimum(0, low_y[0])
         product(3, 0, PASSES, "raw1_1")
         gather(1, 1, "raw3_0")
         whole_row(0)
-        fetch_scores(2, low_y[2], 0, "raw3_1")
-        weigh(1, "raw2_1", 1)
+        weigh(1, None, 1)
+        fetch_scores(2, 0, "raw3_1")
         invert(0)
-        join(1, "neg_max0")
-        new_result(0, "raw2_1")
+        join(1)
+        new_result(0, "weighed1")
         normalise_on_gpsimd(0)
         store(0)
         gather(2, 0)
         gather(2, 1)
-        fetch_scores(3, None, 0, "raw1_0")
-        minimum(1, low_y[1])
+        fetch_scores(3, 0, "raw1_0")
+        minimum(1, "h_codes3")
         gather(3, 1)
         whole_row(1)
-        total_y = column("total_y")
-        new_probs(last, "low_y1")
-        exponentials(last, slice(0, S), logits[last][:, low], total_y)
         weigh(2, "grouped2")
+        total_y = column("total_y")
+        new_probs(last, "fetched2")
+        exponentials(last, slice(0, S), logits[last][:, low], total_y)
         mix(3, 0)
         join(2)
         invert(1)
         new_result(1, "grouped2")
-        normalise_on_gpsimd(1)
+        normalise_on_gpsimd(1, (S + R) // 2)
+        normalise_on_scalar(1, (S + R) // 2)
         store(1)
-        weigh(3, "neg_max1", 1)
-        minimum(2, low_y[2])
+        weigh(3, "h_codes3", 1)
+        minimum(2, "logits1")
         total_y_less_one = column("others")
         whole_row(2)
         nc.scalar.activation(out=total_y_less_one, in_=total_y, func=ACT.Copy, bias=-1.0)
         join(3)
-        neg_max[last] = column("neg_max3")
-        nc.vector.tensor_reduce(
-            out=neg_max[last], in_=logits[last][:, S : S + R + 1], axis=mybir.AxisListType.X, op=ALU.min
-        )
+        minimum(3)
         syn_and_low = slice(S, S + R + 1)
         total_syn_and_factor = column("total_syn")
         exponentials(last, syn_and_low, neg_max[last], total_syn_and_factor)

@@ -243,14 +243,14 @@ def tile_picked_ymochi_soft_p_kernel(
         def new_result(i, tag=None):
             result[i] = wide(f"result{i}", S + R, tag)
 
-        def normalise_on_gpsimd(i, end=S + R):
+        def normalise_on_gpsimd(i, first, end):
             nc.gpsimd.tensor_scalar(
-                out=result[i][:, :end], in0=probs[i][:, :end], scalar1=inv_total[i], scalar2=0.0, op0=ALU.mult, op1=ALU.add
+                out=result[i][:, first:end], in0=probs[i][:, first:end], scalar1=inv_total[i], scalar2=0.0, op0=ALU.mult, op1=ALU.add
             )
 
-        def normalise_on_scalar(i, first):
+        def normalise_on_scalar(i, first, end=S + R):
             nc.scalar.activation(
-                out=result[i][:, first:], in_=probs[i][:, first : S + R], func=ACT.Copy, scale=inv_total[i]
+                out=result[i][:, first:end], in_=probs[i][:, first:end], func=ACT.Copy, scale=inv_total[i]
             )
 
         def normalise_on_vector(i):
@@ -277,7 +277,7 @@ def tile_picked_ymochi_soft_p_kernel(
         invert(0)
         join(1)
         new_result(0, "weighed1")
-        normalise_on_gpsimd(0)
+        normalise_on_gpsimd(0, 0, S + R)
         store(0)
         gather(2, 0)
         gather(2, 1)
@@ -292,16 +292,20 @@ def tile_picked_ymochi_soft_p_kernel(
         mix(3, 0)
         join(2)
         invert(1)
-        new_result(1, "grouped2")
-        normalise_on_gpsimd(1, (S + R) // 2)
-        normalise_on_scalar(1, (S + R) // 2)
-        store(1)
+        new_result(1)
+        normalise_on_scalar(1, 0, S)
+        nc.sync.dma_start(out=out[P : 2 * P, :S], in_=result[1][:, :S])
         weigh(3, "h_codes3", 1)
         minimum(2, "logits1")
         total_y_less_one = column("others")
         whole_row(2)
         nc.scalar.activation(out=total_y_less_one, in_=total_y, func=ACT.Copy, bias=-1.0)
         join(3)
+        syn_result = wide("syn_result1", R, "fetched3")
+        nc.vector.tensor_scalar(
+            out=syn_result[:], in0=probs[1][:, S : S + R], scalar1=inv_total[1], scalar2=None, op0=ALU.mult
+        )
+        nc.sync.dma_start(out=out[P : 2 * P, S:], in_=syn_result[:])
         minimum(3)
         syn_and_low = slice(S, S + R + 1)
         total_syn_and_factor = column("total_syn")

@@ -173,13 +173,13 @@ def tile_picked_ymochi_soft_p_kernel(
         def column(name, tag=None):
             return keep.tile([P, 1], F32, name=name, tag=tag or name, align_bytes=64)[:]
 
-        def fetch_scores(i, half=0, tag=None):
+        def fetch_scores(i, half=0, tag=None, low_y=None):
             if half == 0:
                 logits[i] = keep.tile([P, S + R + PAD], F32, name=f"logits{i}", tag=tag or f"logits{i}", align_bytes=64)
             first, end = spans[i][half]
             nc.vector.tensor_scalar(
                 out=logits[i][:, first:end], in0=banks[i, first][:], scalar1=-1.0, scalar2=None,
-                op0=ALU.mult, op1=ALU.min, accum_out=logits[i][:, S + R + half : S + R + half + 1],
+                op0=ALU.mult, op1=ALU.min, accum_out=logits[i][:, low] if low_y is None else low_y,
             )
 
         def wide(name, columns, tag=None):
@@ -217,7 +217,7 @@ def tile_picked_ymochi_soft_p_kernel(
         def minimum(i, tag=None):
             neg_max[i] = column(f"neg_max{i}", tag)
             nc.vector.tensor_reduce(
-                out=neg_max[i], in_=logits[i][:, S : S + R + len(spans[i])], axis=mybir.AxisListType.X, op=ALU.min
+                out=neg_max[i], in_=logits[i][:, S : S + R + 1], axis=mybir.AxisListType.X, op=ALU.min
             )
 
         def exponentials(i, columns, bias, accum):
@@ -258,16 +258,21 @@ def tile_picked_ymochi_soft_p_kernel(
                 out=result[i][:], in0=probs[i][:, : S + R], scalar1=inv_total[i], scalar2=None, op0=ALU.mult
             )
 
-        fetch_scores(0, 0, "raw1_0")
+        fetch_scores(0, 0)
         product(1, 0, 1, "scales_d")
-        fetch_scores(0, 1)
+        second_low = column("second_low", "raw1_0")
+        fetch_scores(0, 1, None, second_low)
         product(1, 1, 2, "scales_b")
         mix(0, 0, "raw1_1")
         mix(0, 1, "grouped1")
         fetch_scores(1)
         join(0)
         product(2, 0, PASSES, "scales_b")
-        minimum(0)
+        neg_max[0] = column("neg_max0")
+        nc.vector.tensor_scalar(
+            out=logits[0][:, S : S + R + 1], in0=logits[0][:, S : S + R + 1], scalar1=1.0, scalar2=second_low,
+            op0=ALU.mult, op1=ALU.min, accum_out=neg_max[0],
+        )
         mix(1, 0, "grouped2")
         product(3, 0, PASSES, "raw1_1")
         gather(1, 1, "raw3_0")
@@ -281,32 +286,33 @@ def tile_picked_ymochi_soft_p_kernel(
         store(0)
         gather(2, 0)
         gather(2, 1)
-        fetch_scores(3, 0, "raw1_0")
+        fetch_scores(3, 0, "logits0")
         minimum(1, "h_codes3")
         gather(3, 1)
         whole_row(1)
         weigh(2, "grouped2")
         total_y = column("total_y")
-        new_probs(last, "fetched2")
+        new_probs(last, "h_codes3")
         exponentials(last, slice(0, S), logits[last][:, low], total_y)
-        mix(3, 0)
+        weigh(3, None, 1)
         join(2)
+        mix(3, 0, "fetched2")
+        minimum(2)
         invert(1)
-        new_result(1)
-        normalise_on_scalar(1, 0, S)
-        nc.sync.dma_start(out=out[P : 2 * P, :S], in_=result[1][:, :S])
-        weigh(3, "h_codes3", 1)
-        minimum(2, "logits1")
         total_y_less_one = column("others")
         whole_row(2)
         nc.scalar.activation(out=total_y_less_one, in_=total_y, func=ACT.Copy, bias=-1.0)
         join(3)
-        syn_result = wide("syn_result1", R, "fetched3")
+        new_result(1, "grouped2")
         nc.vector.tensor_scalar(
-            out=syn_result[:], in0=probs[1][:, S : S + R], scalar1=inv_total[1], scalar2=None, op0=ALU.mult
+            out=result[1][:, :S], in0=probs[1][:, :S], scalar1=inv_total[1], scalar2=None, op0=ALU.mult
         )
-        nc.sync.dma_start(out=out[P : 2 * P, S:], in_=syn_result[:])
+        nc.sync.dma_start(out=out[P : 2 * P, :S], in_=result[1][:, :S])
         minimum(3)
+        nc.vector.tensor_scalar(
+            out=result[1][:, S:], in0=probs[1][:, S : S + R], scalar1=inv_total[1], scalar2=None, op0=ALU.mult
+        )
+        nc.sync.dma_start(out=out[P : 2 * P, S:], in_=result[1][:, S:])
         syn_and_low = slice(S, S + R + 1)
         total_syn_and_factor = column("total_syn")
         exponentials(last, syn_and_low, neg_max[last], total_syn_and_factor)

from contextlib import ExitStack

import concourse.mybir as mybir
from concourse.masks import make_identity

K, T, S, V, R = 1024, 2048, 512, 512, 256
P = 128
PACK = 4
K_PASS = P * PACK
PASSES = K // K_PASS
TILES = V // P
QUADS = 4
SCALE_ROWS = 4
RUN = 4
PER = R // P
PAD = 8
FLOPS = 2 * K * V * S

F32 = mybir.dt.float32
BF16 = mybir.dt.bfloat16
I32 = mybir.dt.int32
U32 = mybir.dt.uint32
U16 = mybir.dt.uint16
U8 = mybir.dt.uint8
FP8X4 = mybir.dt.float8_e4m3fn_x4
ALU = mybir.AluOpType
ACT = mybir.ActivationFunctionType


def tile_picked_ymochi_soft_p_kernel(
    tc, x_words, x_scales, hT, share, inv, offs, one, two, out
):
    nc = tc.nc
    with ExitStack() as ctx:
        keep = ctx.enter_context(tc.tile_pool(name="keep", bufs=1))
        psum = ctx.enter_context(tc.psum_pool(name="psum", bufs=1))
        pairs = [(i, o) for i in range(TILES) for o in range(PASSES)]

        offs_t = keep.tile([P, S // 16], U16, name="offs_t")
        one_t = keep.tile([P, R // 16], U16, name="one_t")
        two_t = keep.tile([P, R // 16], U16, name="two_t")
        words = [keep.tile([P, T], I32, name=f"words{o}", align_bytes=64) for o in range(PASSES)]
        scale_rows = keep.tile([P, T], U8, name="scale_rows", align_bytes=64)
        share_t = keep.tile([P, PER], F32, name="share_t")
        inv_t = keep.tile([P, PER], F32, name="inv_t", align_bytes=64)
        raw = {(i, o): keep.tile([P, PACK, P], F32, name=f"raw{i}_{o}", align_bytes=64) for i, o in pairs}

        def load_words(o):
            nc.sync.dma_start(out=words[o][:], in_=x_words[o].rearrange("p n t -> p (n t)").bitcast(I32))

        def load_queries(i, o, queue=nc.sync):
            rows = hT[o * K_PASS : (o + 1) * K_PASS, i * P : (i + 1) * P]
            queue.dma_start(out=raw[i, o][:], in_=rows.rearrange("(p j) q -> p j q", j=PACK))

        landed_rows = keep.tile([P, T], U8, name="landed_rows", align_bytes=64)
        live = [slice(32 * quad, 32 * quad + SCALE_ROWS * PASSES) for quad in range(QUADS)]
        for quad in range(QUADS):
            (nc.scalar if quad < QUADS // 2 else nc.sync).dma_start(
                out=landed_rows[live[quad], :].bitcast(I32),
                in_=x_scales[:, SCALE_ROWS * quad : SCALE_ROWS * (quad + 1), :].bitcast(I32),
            )
        nc.sync.dma_start(out=offs_t[:], in_=offs)
        load_words(0)
        for tile, rows in ((share_t, share), (inv_t, inv)):
            nc.scalar.dma_start(out=tile[:], in_=rows[0, :].rearrange("(p c) -> p c", p=P))
        for o in range(PASSES):
            load_queries(0, o, nc.scalar)
        load_words(1)
        nc.sync.dma_start(out=one_t[:], in_=one)
        nc.sync.dma_start(out=two_t[:], in_=two)
        for i in range(1, TILES):
            for o in range(PASSES):
                load_queries(i, o)

        identity = keep.tile([P, P], F32, name="identity")
        make_identity(nc, identity[:])
        columns_w = keep.tile([P, 2 * PER], F32, name="columns_w")
        nc.vector.tensor_tensor(out=columns_w[:, :PER], in0=share_t[:], in1=inv_t[:], op=ALU.mult)
        nc.vector.scalar_tensor_tensor(
            out=columns_w[:, PER:], in0=share_t[:], scalar=1.0, in1=inv_t[:], op0=ALU.subtract, op1=ALU.mult
        )
        spread = psum.tile([P, 2 * PER, P], F32, name="spread")
        for n in range(2 * PER):
            nc.tensor.transpose(spread[:, n, :], columns_w[:, n : n + 1].to_broadcast([P, P]), identity[:])
        weights = keep.tile([P, 2 * R], F32, name="weights")
        nc.scalar.copy(
            out=weights[:].rearrange("q (t p c) -> q t p c", t=2, c=PER),
            in_=spread[:].rearrange("q (t c) p -> q t p c", t=2),
        )
        w_one = weights[:, :R]
        w_two = weights[:, R:]

        picked_scales = keep.tile([P, S], U8, name="picked_scales", align_bytes=64)
        picked = {}
        nc.vector.memset(scale_rows[:].bitcast(I32), 0)
        for quad in range(QUADS):
            nc.vector.tensor_copy(out=scale_rows[live[quad], :].bitcast(I32), in_=landed_rows[live[quad], :].bitcast(I32))
        nc.vector.tensor_copy(out=picked_scales[:], in_=scale_rows[:].indirect(offs_t[:]))

        def pick_words(o, pieces, tag):
            picked[o] = keep.tile([P, S], U32, name=f"picked{o}", tag=tag, align_bytes=64)
            for first, end in pieces:
                nc.vector.tensor_copy(
                    out=picked[o][:, first:end],
                    in_=words[o][:].bitcast(U32).indirect(offs_t[:, first // 16 : end // 16]),
                )

        pick_words(0, [(0, S)], "picked0")

        grouped = [keep.tile([P, PASSES * K_PASS], BF16, name=f"grouped{i}", align_bytes=64) for i in range(TILES)]
        h_codes = {}
        h_scales = {}
        spans = {i: [(0, S // 2), (S // 2, S)] if i == 0 else [(0, S)] for i in range(TILES)}
        banks = {
            (i, first): psum.tile([P, end - first], F32, name=f"bank{i}_{first}")
            for i in range(TILES)
            for first, end in spans[i]
        }

        def interleave(copy, i, o, first, end):
            copy(
                out=grouped[i][:, o * K_PASS + PACK * first : o * K_PASS + PACK * end].rearrange(
                    "p (c n j) -> p c j n", n=RUN, j=PACK
                ),
                in_=raw[i, o][:, :, first:end].rearrange("p j (c n) -> p c j n", n=RUN),
            )

        def quantise(i, first, end, tag):
            scales = keep.tile([P, (end - first) * P], U8, name=f"h_scales{i}_{first}", tag=tag, align_bytes=64)
            name = f"h_codes{i}" if end == PASSES else f"early_codes{i}"
            codes = keep.tile([P, (end - first) * P], U32, name=name, align_bytes=64)
            for o in range(first, end):
                h_codes[i, o] = codes[:, (o - first) * P : (o - first + 1) * P]
                h_scales[i, o] = scales[:, (o - first) * P : (o - first + 1) * P]
            nc.vector.quantize_mx(
                out=codes[:].bitcast(FP8X4), scales=scales[:], in_=grouped[i][:, first * K_PASS : end * K_PASS]
            )

        def multiply(i, o):
            for first, end in spans[i]:
                nc.tensor.matmul_mx(
                    out=banks[i, first][:],
                    lhsT=h_codes[i, o].bitcast(FP8X4),
                    lhsT_scale=h_scales[i, o],
                    rhs=picked[o][:, first:end].bitcast(FP8X4),
                    rhs_scale=picked_scales[SCALE_ROWS * o :, first:end],
                    start=(o == 0),
                    stop=(o == PASSES - 1),
                )

        def product(i, first, end, tag):
            quantise(i, first, end, tag)
            for o in range(first, end):
                multiply(i, o)

        for i, o in pairs:
            interleave(nc.scalar.copy, i, o, 0, P)
        product(0, 0, 1, "scales_a")
        quantise(0, 1, 2, "scales_b")
        pick_words(1, spans[0], "grouped0")
        multiply(0, 1)

        last = TILES - 1
        low = slice(S + R, S + R + 1)
        logits = {}
        parts = {}
        probs = {}
        neg_max = {}
        total = {}
        inv_total = {}
        result = {}

        def column(name, tag=None):
            return keep.tile([P, 1], F32, name=name, tag=tag or name, align_bytes=64)[:]

        def fetch_scores(i, half=0, tag=None, low_y=None):
            if half == 0:
                logits[i] = keep.tile([P, S + R + PAD], F32, name=f"logits{i}", tag=tag or f"logits{i}", align_bytes=64)
            first, end = spans[i][half]
            nc.vector.tensor_scalar(
                out=logits[i][:, first:end], in0=banks[i, first][:], scalar1=-1.0, scalar2=None,
                op0=ALU.mult, op1=ALU.min, accum_out=logits[i][:, low] if low_y is None else low_y,
            )

        def wide(name, columns, tag=None):
            return keep.tile([P, columns], F32, name=name, tag=tag or name, align_bytes=64)

        def mix(i, n, tag=None):
            parts[i, n] = wide(f"part{i}_{n}", R, tag)[:]
            nc.vector.tensor_tensor(
                out=parts[i, n], in0=logits[i][:].indirect((one_t, two_t)[n][:]), in1=(w_one, w_two)[n], op=ALU.mult
            )

        fetched = {}

        def gather(i, n, tag=None):
            if i not in fetched:
                fetched[i] = wide(f"fetched{i}", 2 * R, tag)
            nc.scalar.activation(
                out=fetched[i][:, n * R : (n + 1) * R], in_=logits[i][:].indirect((one_t, two_t)[n][:]), func=ACT.Copy
            )

        def weigh(i, tag=None, first=0):
            weighed = wide(f"weighed{i}", 2 * R, tag)
            nc.vector.tensor_tensor(
                out=weighed[:, first * R :].rearrange("q (t p c) -> q t p c", p=P, c=PER),
                in0=fetched[i][:, first * R :].rearrange("q (t p c) -> q t p c", p=P, c=PER),
                in1=spread[:, first * PER :, :].rearrange("q (t c) p -> q t p c", c=PER),
                op=ALU.mult,
            )
            for n in range(first, 2):
                parts[i, n] = weighed[:, n * R : (n + 1) * R]

        def join(i):
            nc.vector.tensor_tensor(out=logits[i][:, S : S + R], in0=parts[i, 0], in1=parts[i, 1], op=ALU.subtract)

        def minimum(i, tag=None):
            neg_max[i] = column(f"neg_max{i}", tag)
            nc.vector.tensor_reduce(
                out=neg_max[i], in_=logits[i][:, S : S + R + 1], axis=mybir.AxisListType.X, op=ALU.min
            )

        def exponentials(i, columns, bias, accum):
            nc.scalar.activation(
                out=probs[i][:, columns], in_=logits[i][:, columns], func=ACT.Exp, bias=bias, scale=-1.0, accum_out=accum
            )

        def new_probs(i, tag=None):
            probs[i] = wide(f"probs{i}", S + R + PAD, tag)

        def whole_row(i, tag=None):
            new_probs(i, tag)
            total[i] = column(f"total{i}")
            exponentials(i, slice(0, S + R), neg_max[i], total[i])

        def invert(i):
            inv_total[i] = column(f"inv_total{i}")
            nc.vector.reciprocal(out=inv_total[i], in_=total[i])

        def store(i):
            nc.sync.dma_start(out=out[i * P : (i + 1) * P, :], in_=result[i][:])

        def new_result(i, tag=None):
            result[i] = wide(f"result{i}", S + R, tag)

        def normalise_on_gpsimd(i, first, end):
            nc.gpsimd.tensor_scalar(
                out=result[i][:, first:end], in0=probs[i][:, first:end], scalar1=inv_total[i], scalar2=0.0, op0=ALU.mult, op1=ALU.add
            )

        def normalise_on_scalar(i, first, end=S + R):
            nc.scalar.activation(
                out=result[i][:, first:end], in_=probs[i][:, first:end], func=ACT.Copy, scale=inv_total[i]
            )

        def normalise_on_vector(i):
            nc.vector.tensor_scalar(
                out=result[i][:], in0=probs[i][:, : S + R], scalar1=inv_total[i], scalar2=None, op0=ALU.mult
            )

        fetch_scores(0, 0)
        product(1, 0, 1, "scales_d")
        second_low = column("second_low", "raw1_0")
        fetch_scores(0, 1, None, second_low)
        product(1, 1, 2, "scales_b")
        mix(0, 0, "raw1_1")
        mix(0, 1, "grouped1")
        fetch_scores(1)
        join(0)
        product(2, 0, PASSES, "scales_b")
        neg_max[0] = column("neg_max0")
        nc.vector.tensor_scalar(
            out=logits[0][:, S : S + R + 1], in0=logits[0][:, S : S + R + 1], scalar1=1.0, scalar2=second_low,
            op0=ALU.mult, op1=ALU.min, accum_out=neg_max[0],
        )
        mix(1, 0, "grouped2")
        product(3, 0, PASSES, "raw1_1")
        gather(1, 1, "raw3_0")
        whole_row(0)
        weigh(1, None, 1)
        fetch_scores(2, 0, "raw3_1")
        invert(0)
        join(1)
        new_result(0, "weighed1")
        normalise_on_gpsimd(0, 0, S + R)
        store(0)
        gather(2, 0)
        gather(2, 1)
        fetch_scores(3, 0, "logits0")
        minimum(1, "h_codes3")
        gather(3, 1)
        whole_row(1)
        weigh(2, "grouped2")
        total_y = column("total_y")
        new_probs(last, "h_codes3")
        exponentials(last, slice(0, S), logits[last][:, low], total_y)
        weigh(3, None, 1)
        join(2)
        mix(3, 0, "fetched2")
        minimum(2)
        invert(1)
        total_y_less_one = column("others")
        whole_row(2)
        nc.scalar.activation(out=total_y_less_one, in_=total_y, func=ACT.Copy, bias=-1.0)
        join(3)
        new_result(1, "grouped2")
        nc.vector.tensor_scalar(
            out=result[1][:, :S], in0=probs[1][:, :S], scalar1=inv_total[1], scalar2=None, op0=ALU.mult
        )
        nc.sync.dma_start(out=out[P : 2 * P, :S], in_=result[1][:, :S])
        minimum(3)
        nc.vector.tensor_scalar(
            out=result[1][:, S:], in0=probs[1][:, S : S + R], scalar1=inv_total[1], scalar2=None, op0=ALU.mult
        )
        nc.sync.dma_start(out=out[P : 2 * P, S:], in_=result[1][:, S:])
        syn_and_low = slice(S, S + R + 1)
        total_syn_and_factor = column("total_syn")
        exponentials(last, syn_and_low, neg_max[last], total_syn_and_factor)
        invert(2)
        new_result(2)
        normalise_on_vector(2)
        store(2)
        factor = probs[last][:, low]
        total[last] = column("total3")
        nc.scalar.activation(
            out=total[last], in_=factor, func=ACT.Identity, scale=total_y_less_one, bias=total_syn_and_factor
        )
        invert(last)
        new_result(last)
        nc.vector.tensor_scalar(
            out=result[last][:, :S], in0=probs[last][:, :S], scalar1=inv_total[last], scalar2=factor,
            op0=ALU.mult, op1=ALU.mult,
        )
        normalise_on_scalar(last, S)
        store(last)
